import numpy as np
import ml_dtypes


def mxq(x, axis, fmt="e4m3"):
    dtype, down = {"e4m3": (ml_dtypes.float8_e4m3fn, 7), "e5m2": (ml_dtypes.float8_e5m2, 14)}[fmt]
    v = np.moveaxis(np.asarray(x, np.float32).astype(ml_dtypes.bfloat16).astype(np.float64), axis, -1)
    blocks = v.reshape(v.shape[:-1] + (-1, 32))
    amax = np.abs(blocks).max(-1, keepdims=True)
    byte = np.maximum(np.where(amax > 0, np.frexp(amax)[1] - 1 + 127, 0) - down, 1)
    scale = np.exp2(byte - 127.0)
    codes = (blocks / scale).astype(np.float32).astype(dtype).astype(np.float64)
    return np.moveaxis((codes * scale).reshape(v.shape), -1, axis)


WIDE = False


def mx_kscale(k):
    if not WIDE:
        return np.ones(k)
    levels = np.array([10, -10, 5, -5, 0])
    if k % 512:
        return np.exp2(np.random.permutation(np.resize(levels, k // 32))).repeat(32)
    a = np.empty((k // 512, 16))
    for p in range(k // 512):
        a[p, :8] = np.random.permutation(np.resize(levels, 8))
        for g in range(8):
            far = levels[np.abs(levels - a[p, g]) >= 10]
            a[p, g + 8] = far[np.random.randint(len(far))]
    return np.exp2(a.ravel()).repeat(32)


def f64(x):
    return np.asarray(x).astype(np.float64)


def striped(idx):
    return np.tile(idx.reshape(-1, 16).T, (8, 1)).astype(np.uint16)


def unstriped(offs):
    return offs[:16].T.reshape(-1).astype(np.int64)


def pack_weight(w):
    k, n = w.shape
    w = f64(np.asarray(w, np.float32).astype(ml_dtypes.bfloat16)).reshape(k // 32, 32, n)
    amax = np.abs(w).max(1)
    byte = np.clip(np.where(amax > 0, np.frexp(amax)[1] - 1 + 127 - 7, 1), 1, 254)
    scaled = (w * np.exp2(127.0 - byte)[:, None, :]).reshape(k, n).astype(np.float32)
    words = np.ascontiguousarray(scaled.reshape(k // 512, 128, 4, n).transpose(0, 1, 3, 2)).astype(ml_dtypes.float8_e4m3fn).view(np.uint8)
    return words, np.ascontiguousarray(byte.astype(np.uint8).reshape(k // 512, 16, n))


def unpack_weight(words, scales):
    g, p, n, _ = words.shape
    vals = np.ascontiguousarray(words).view(ml_dtypes.float8_e4m3fn).astype(np.float64) * np.repeat(np.exp2(scales.astype(np.float64) - 127.0), 8, axis=1)[..., None]
    return vals.transpose(0, 1, 3, 2).reshape(g * 512, n)


def planes(y):
    n, m = y.shape
    v = y.astype(np.float32).astype(ml_dtypes.bfloat16).astype(np.float64).reshape(n // 32, 32, m)
    top = np.abs(v).max(1)
    byte = np.clip(np.where(top > 0, np.frexp(top)[1] - 1 + 127 - 7, 1), 1, 254)
    codes = (v * np.exp2(127.0 - byte)[:, None, :]).reshape(n, m).astype(np.float32).astype(ml_dtypes.float8_e4m3fn).view(np.uint8)
    words = codes.reshape(n // 512, 128, 4, m).transpose(0, 1, 3, 2)
    return np.ascontiguousarray(words), np.ascontiguousarray(byte.astype(np.uint8).reshape(n // 512, 16, m))


K, T, S, H, N, U = 1024, 2048, 512, 512, 512, 1024


def setup_inputs():
    n = np.random.standard_normal
    s = mx_kscale(K)[:, None]
    u = mx_kscale(H)
    packed_xT = pack_weight(n((K, T)) * s)
    return {
        "x_words": packed_xT[0],
        "x_scales": packed_xT[1],
        "mom": (n((N, U))).astype(np.float32),
        "w1": (n((K, N)) / np.sqrt(K) / s).astype(np.float32),
        "w2": (n((H, N)) / np.sqrt(H) / u[:, None]).astype(np.float32),
        "bias": (0.5 * n((H, 1))).astype(np.float32),
        "top": (n((H, 1)) * u[:, None]).astype(np.float32),
        "offs": striped(np.random.permutation(T)[:S]),
        "slot": striped(np.random.permutation(U)[:S]),
    }


def reference(x_words, x_scales, mom, w1, w2, bias, top, offs, slot):
    xq = unpack_weight(x_words, x_scales)[:, unstriped(offs)]
    h = np.tanh((mxq(f64(w1), 0, "e4m3").T @ xq) + f64(bias))
    z = f64(top) * (-1.0 * ((h) ** 2) + 1.0)
    p = f64(mom)[:, unstriped(slot)] - (0.2 * ((mxq(f64(w2), 0, "e4m3").T @ mxq(z, 0, "e4m3"))))
    out = f64(mom).copy()
    out[:, unstriped(slot)] = p
    out_0 = out
    return (out_0,) + planes(out_0)

@@ -1,0 +1,226 @@
+from contextlib import ExitStack
+
+import concourse.mybir as mybir
+
+K, T, S, H, N, U = 1024, 2048, 512, 512, 512, 1024
+FLOPS = 2 * K * H * S + 2 * H * N * S
+
+F32 = mybir.dt.float32
+BF16 = mybir.dt.bfloat16
+I32 = mybir.dt.int32
+U32 = mybir.dt.uint32
+U16 = mybir.dt.uint16
+U8 = mybir.dt.uint8
+FP8X4 = mybir.dt.float8_e4m3fn_x4
+ALU = mybir.AluOpType
+ACT = mybir.ActivationFunctionType
+
+P = 128
+PACK = 4
+PASSES = K // (P * PACK)
+HALF = S // 2
+COLS = U // 2
+
+
+def tile_picked_yham_euler_po_kernel(
+    tc, x_words, x_scales, mom, w1, w2, bias, top, offs, slot, out_0, out_1, out_2
+):
+    nc = tc.nc
+    with ExitStack() as ctx:
+        keep = ctx.enter_context(tc.tile_pool(name="keep", bufs=1))
+        psum = ctx.enter_context(tc.psum_pool(name="psum", bufs=8))
+
+        def sb(name, shape, dtype, tag=None):
+            return keep.tile(shape, dtype, name=name, tag=tag or name, align_bytes=64)
+
+        offs_sb = keep.tile([P, S // 16], U16, name="offs_sb")
+        slot_sb = keep.tile([P, S // 16], U16, name="slot_sb")
+        xs_win = sb("xs_win", [P, T], U8)
+        xw_win = [sb(f"xw_win{g}", [P, T], U32) for g in range(PASSES)]
+        w1_raw = [sb(f"w1_raw{g}", [P, PACK, H], F32) for g in range(PASSES)]
+        w2_raw = sb("w2_raw", [P, PACK, N], F32)
+        y = [sb(f"y{t}", [P, U], F32) for t in range(PACK)]
+        bias_sb = sb("bias_sb", [P, PACK], F32)
+        top_sb = sb("top_sb", [P, PACK], F32)
+        ntop = sb("ntop", [P, PACK], F32)
+        warm_in = sb("warm_in", [P, 1], F32)
+        warm_out = sb("warm_out", [P, 1], F32)
+
+        mom_rows = mom.rearrange("(p t) c -> t p c", t=PACK)
+        out_rows = out_0.rearrange("(p t) c -> t p c", t=PACK)
+
+        nc.vector.memset(xs_win[:].bitcast(I32), 0)
+        nc.vector.memset(warm_in[:], 0.0)
+        nc.scalar.activation(warm_out[:], warm_in[:], ACT.Tanh)
+
+        nc.sync.dma_start(offs_sb[:], offs)
+        for g in range(PASSES):
+            nc.sync.dma_start(w1_raw[g][:], w1[g * 512:(g + 1) * 512, :].rearrange("(p j) c -> p j c", j=PACK))
+            if g == 0:
+                for q in range(4):
+                    nc.sync.dma_start(xs_win[32 * q:32 * q + 8, :].bitcast(I32), x_scales[:, 4 * q:4 * q + 4, :].bitcast(I32))
+        nc.sync.dma_start(bias_sb[:], bias.rearrange("(p t) o -> p (t o)", t=PACK))
+        nc.sync.dma_start(top_sb[:], top.rearrange("(p t) o -> p (t o)", t=PACK))
+        nc.sync.dma_start(slot_sb[:], slot)
+        nc.sync.dma_start(w2_raw[:], w2.rearrange("(p j) c -> p j c", j=PACK))
+        for g in range(PASSES):
+            nc.sync.dma_start(xw_win[g][:].bitcast(I32), x_words[g].rearrange("p c r -> p (c r)").bitcast(I32))
+        for t in range(PACK):
+            nc.sync.dma_start(y[t][:], mom_rows[t])
+
+        def deal(raw, name, copy):
+            grouped = sb(name, [P, PACK, P, PACK], BF16)
+            copy(grouped[:].rearrange("p t m j -> p m j t"), raw[:].rearrange("p j (m t) -> p m j t", t=PACK))
+            return grouped
+
+        def quant(grouped2d, name, width):
+            codes = sb(name + "_c", [P, width], U32)
+            scales = sb(name + "_s", [P, width], U8)
+            nc.vector.quantize_mx(out=codes[:].bitcast(FP8X4), scales=scales[:], in_=grouped2d)
+            return codes, scales
+
+        w1q = []
+        xs = sb("xs", [P, S], U8)
+        for g in range(PASSES):
+            grouped = deal(w1_raw[g], f"w1_g{g}", nc.vector.tensor_copy if g == 0 else nc.scalar.copy)
+            w1q.append(quant(grouped[:].rearrange("p t m j -> p (t m j)"), f"w1q{g}", H))
+            if g == 0:
+                nc.vector.tensor_copy(xs[:], xs_win[:].indirect(offs_sb[:]))
+
+        nc.scalar.activation(ntop[:], top_sb[:], ACT.Copy, scale=-1.0)
+        w2_g = deal(w2_raw, "w2_g", nc.vector.tensor_copy)
+        w2q = quant(w2_g[:].rearrange("p t m j -> p (t m j)"), "w2q", N)
+        xw = {}
+        acc1 = {}
+        for g in range(PASSES):
+            for hf in range(2):
+                xw[g, hf] = sb(f"xw{g}{hf}", [P, HALF], U32)
+                nc.vector.tensor_copy(xw[g, hf][:], xw_win[g][:].indirect(offs_sb[:, hf * 16:(hf + 1) * 16]))
+                for t in range(PACK):
+                    if g == 0:
+                        acc1[hf, t] = psum.tile([P, HALF], F32, name="acc")
+                    nc.tensor.matmul_mx(
+                        out=acc1[hf, t][:],
+                        lhsT=w1q[g][0][:, t * P:(t + 1) * P].bitcast(FP8X4),
+                        lhsT_scale=w1q[g][1][:, t * P:(t + 1) * P],
+                        rhs=xw[g, hf][:].bitcast(FP8X4),
+                        rhs_scale=xs[4 * g:P, hf * HALF:(hf + 1) * HALF],
+                        start=(g == 0),
+                        stop=(g == PASSES - 1),
+                    )
+
+        pieces = [(0, 128), (128, 256), (256, 512)]
+        old = {}
+        kick = [sb(f"kick{t}", [P, S], F32) for t in range(PACK)]
+
+        def fetch_old(t, tag):
+            old[t] = sb(f"old{t}", [P, S], F32, tag=tag)
+            nc.vector.tensor_copy(old[t][:], y[t][:].indirect(slot_sb[:]))
+
+        def tanh(i):
+            lo, hi = pieces[i]
+            h = sb(f"h{i}", [P, PACK, hi - lo], F32)
+            for t in range(PACK):
+                src = acc1[lo // HALF, t][:, lo % HALF:lo % HALF + hi - lo]
+                nc.scalar.activation(h[:, t, :], src, ACT.Tanh, bias=bias_sb[:, t:t + 1])
+            return h
+
+        def square(i, h):
+            lo, hi = pieces[i]
+            sq = sb(f"sq{i}", [P, hi - lo, PACK], F32)
+            nc.scalar.activation(
+                sq[:].rearrange("p (c i) t -> p c t i", i=4), h[:].rearrange("p t (c i) -> p c t i", i=4), ACT.Square
+            )
+            return sq
+
+        def slope(i, sq):
+            lo, hi = pieces[i]
+            z = sb(f"z{i}", [P, hi - lo, PACK], BF16)
+            nc.vector.scalar_tensor_tensor(
+                z[:], sq[:], 1.0, ntop[:].unsqueeze(1).to_broadcast([P, hi - lo, PACK]), ALU.subtract, ALU.mult
+            )
+            return z
+
+        z_codes = sb("z_codes", [P, S], U32)
+        z_scales = sb("z_scales", [P, S], U8)
+
+        def zquant(i, z):
+            lo, hi = pieces[i]
+            nc.vector.quantize_mx(
+                out=z_codes[:, lo:hi].bitcast(FP8X4), scales=z_scales[:, lo:hi], in_=z[:].rearrange("p c t -> p (c t)")
+            )
+
+        def second(lo, hi, ts):
+            for t in ts:
+                acc = psum.tile([P, hi - lo], F32, name="acc")
+                nc.tensor.matmul_mx(
+                    out=acc[:],
+                    lhsT=w2q[0][:, t * P:(t + 1) * P].bitcast(FP8X4),
+                    lhsT_scale=w2q[1][:, t * P:(t + 1) * P],
+                    rhs=z_codes[:, lo:hi].bitcast(FP8X4),
+                    rhs_scale=z_scales[:, lo:hi],
+                    start=True,
+                    stop=True,
+                )
+                nc.scalar.activation(kick[t][:, lo:hi], acc[:], ACT.Copy, scale=-0.2)
+
+        def scatter(t, lo, hi):
+            nc.vector.tensor_tensor(
+                y[t][:].indirect(slot_sb[:, lo // 16:hi // 16]), old[t][:, lo:hi], kick[t][:, lo:hi], ALU.add
+            )
+
+        grp = [sb(f"grp{c}", [P, COLS, PACK], BF16) for c in range(2)]
+
+        def finish(t):
+            nc.sync.dma_start(out_rows[t], y[t][:])
+            for c in range(2):
+                src = y[t][:, c * COLS:(c + 1) * COLS]
+                if t == PACK - 1 and c == 0:
+                    nc.vector.tensor_copy(grp[c][:, :, t], src)
+                elif t == PACK - 2 and c == 0:
+                    nc.scalar.copy(grp[c][:, :, t:t + 2], src.unsqueeze(2).to_broadcast([P, COLS, 2]))
+                else:
+                    nc.scalar.copy(grp[c][:, :, t], src)
+
+        sq0 = square(0, tanh(0))
+        fetch_old(0, "old0")
+        sq1 = square(1, tanh(1))
+        zquant(0, slope(0, sq0))
+        fetch_old(1, "sq0")
+        second(*pieces[0], (0, 1))
+        z1 = slope(1, sq1)
+        scatter(0, *pieces[0])
+        zquant(1, z1)
+        scatter(1, *pieces[0])
+        h2 = tanh(2)
+        second(*pieces[1], (0, 1))
+        fetch_old(2, "sq1")
+        z2 = slope(2, square(2, h2))
+        scatter(0, *pieces[1])
+        zquant(2, z2)
+        scatter(1, *pieces[1])
+        second(*pieces[2], (0, 1))
+        second(0, S, (2, 3))
+        fetch_old(3, "sq2")
+        scatter(0, *pieces[2])
+        finish(0)
+        scatter(1, *pieces[2])
+        finish(1)
+        scatter(2, 0, S)
+        finish(2)
+        scatter(3, 0, S)
+        finish(3)
+
+        out_scales = sb("out_scales", [P, U], U8)
+        words = out_1[0].rearrange("p c r -> p (c r)").bitcast(I32)
+        for c in range(2):
+            codes = sb(f"out_codes{c}", [P, COLS], U32)
+            nc.vector.quantize_mx(
+                out=codes[:].bitcast(FP8X4),
+                scales=out_scales[:, c * COLS:(c + 1) * COLS],
+                in_=grp[c][:].rearrange("p c t -> p (c t)"),
+            )
+            nc.sync.dma_start(words[:, c * COLS:(c + 1) * COLS], codes[:].bitcast(I32))
+        for q in range(4):
+            eng = nc.sync if q % 2 == 0 else nc.scalar
+            eng.dma_start(out_2[0, 4 * q:4 * q + 4, :].bitcast(I32), out_scales[32 * q:32 * q + 4, :].bitcast(I32))

@@ -59,18 +59,23 @@ def tile_picked_yham_euler_po_kernel(
             if g == 0:
                 for q in range(4):
                     nc.sync.dma_start(xs_win[32 * q:32 * q + 8, :].bitcast(I32), x_scales[:, 4 * q:4 * q + 4, :].bitcast(I32))
+        for g in range(PASSES):
+            nc.sync.dma_start(xw_win[g][:].bitcast(I32), x_words[g].rearrange("p c r -> p (c r)").bitcast(I32))
         nc.sync.dma_start(bias_sb[:], bias.rearrange("(p t) o -> p (t o)", t=PACK))
         nc.sync.dma_start(top_sb[:], top.rearrange("(p t) o -> p (t o)", t=PACK))
         nc.sync.dma_start(slot_sb[:], slot)
-        nc.sync.dma_start(w2_raw[:], w2.rearrange("(p j) c -> p j c", j=PACK))
-        for g in range(PASSES):
-            nc.sync.dma_start(xw_win[g][:].bitcast(I32), x_words[g].rearrange("p c r -> p (c r)").bitcast(I32))
         for t in range(PACK):
             nc.sync.dma_start(y[t][:], mom_rows[t])
+            if t == 2:
+                nc.sync.dma_start(w2_raw[:], w2.rearrange("(p j) c -> p j c", j=PACK))
 
-        def deal(raw, name, copy):
+        def deal(raw, name, split):
             grouped = sb(name, [P, PACK, P, PACK], BF16)
-            copy(grouped[:].rearrange("p t m j -> p m j t"), raw[:].rearrange("p j (m t) -> p m j t", t=PACK))
+            dst = grouped[:].rearrange("p t m j -> p m j t")
+            src = raw[:].rearrange("p j (m t) -> p m j t", t=PACK)
+            if split > 0:
+                nc.vector.tensor_copy(dst[:, :split], src[:, :split])
+            nc.scalar.copy(dst[:, split:], src[:, split:])
             return grouped
 
         def quant(grouped2d, name, width):
@@ -82,14 +87,11 @@ def tile_picked_yham_euler_po_kernel(
         w1q = []
         xs = sb("xs", [P, S], U8)
         for g in range(PASSES):
-            grouped = deal(w1_raw[g], f"w1_g{g}", nc.vector.tensor_copy if g == 0 else nc.scalar.copy)
+            grouped = deal(w1_raw[g], f"w1_g{g}", 80)
             w1q.append(quant(grouped[:].rearrange("p t m j -> p (t m j)"), f"w1q{g}", H))
             if g == 0:
                 nc.vector.tensor_copy(xs[:], xs_win[:].indirect(offs_sb[:]))
 
-        nc.scalar.activation(ntop[:], top_sb[:], ACT.Copy, scale=-1.0)
-        w2_g = deal(w2_raw, "w2_g", nc.vector.tensor_copy)
-        w2q = quant(w2_g[:].rearrange("p t m j -> p (t m j)"), "w2q", N)
         xw = {}
         acc1 = {}
         for g in range(PASSES):
@@ -109,7 +111,7 @@ def tile_picked_yham_euler_po_kernel(
                         stop=(g == PASSES - 1),
                     )
 
-        pieces = [(0, 128), (128, 256), (256, 512)]
+        pieces = [(0, HALF), (HALF, S)]
         old = {}
         kick = [sb(f"kick{t}", [P, S], F32) for t in range(PACK)]
 
@@ -133,21 +135,12 @@ def tile_picked_yham_euler_po_kernel(
             )
             return sq
 
+        z = sb("z", [P, S, PACK], BF16)
+
         def slope(i, sq):
             lo, hi = pieces[i]
-            z = sb(f"z{i}", [P, hi - lo, PACK], BF16)
             nc.vector.scalar_tensor_tensor(
-                z[:], sq[:], 1.0, ntop[:].unsqueeze(1).to_broadcast([P, hi - lo, PACK]), ALU.subtract, ALU.mult
-            )
-            return z
-
-        z_codes = sb("z_codes", [P, S], U32)
-        z_scales = sb("z_scales", [P, S], U8)
-
-        def zquant(i, z):
-            lo, hi = pieces[i]
-            nc.vector.quantize_mx(
-                out=z_codes[:, lo:hi].bitcast(FP8X4), scales=z_scales[:, lo:hi], in_=z[:].rearrange("p c t -> p (c t)")
+                z[:, lo:hi, :], sq[:], 1.0, ntop[:].unsqueeze(1).to_broadcast([P, hi - lo, PACK]), ALU.subtract, ALU.mult
             )
 
         def second(lo, hi, ts):
@@ -169,58 +162,44 @@ def tile_picked_yham_euler_po_kernel(
                 y[t][:].indirect(slot_sb[:, lo // 16:hi // 16]), old[t][:, lo:hi], kick[t][:, lo:hi], ALU.add
             )
 
-        grp = [sb(f"grp{c}", [P, COLS, PACK], BF16) for c in range(2)]
+        chunks = [(0, 512), (512, 768), (768, 1024)]
+        grp = [sb(f"grp{c}", [P, hi - lo, PACK], BF16) for c, (lo, hi) in enumerate(chunks)]
 
         def finish(t):
             nc.sync.dma_start(out_rows[t], y[t][:])
-            for c in range(2):
-                src = y[t][:, c * COLS:(c + 1) * COLS]
+            for c, (lo, hi) in enumerate(chunks):
+                src = y[t][:, lo:hi]
                 if t == PACK - 1 and c == 0:
                     nc.vector.tensor_copy(grp[c][:, :, t], src)
                 elif t == PACK - 2 and c == 0:
-                    nc.scalar.copy(grp[c][:, :, t:t + 2], src.unsqueeze(2).to_broadcast([P, COLS, 2]))
+                    nc.scalar.copy(grp[c][:, :, t:t + 2], src.unsqueeze(2).to_broadcast([P, hi - lo, 2]))
                 else:
                     nc.scalar.copy(grp[c][:, :, t], src)
 
-        sq0 = square(0, tanh(0))
+        nc.scalar.activation(ntop[:], top_sb[:], ACT.Copy, scale=-1.0)
         fetch_old(0, "old0")
-        sq1 = square(1, tanh(1))
-        zquant(0, slope(0, sq0))
-        fetch_old(1, "sq0")
-        second(*pieces[0], (0, 1))
-        z1 = slope(1, sq1)
-        scatter(0, *pieces[0])
-        zquant(1, z1)
-        scatter(1, *pieces[0])
-        h2 = tanh(2)
-        second(*pieces[1], (0, 1))
-        fetch_old(2, "sq1")
-        z2 = slope(2, square(2, h2))
-        scatter(0, *pieces[1])
-        zquant(2, z2)
-        scatter(1, *pieces[1])
-        second(*pieces[2], (0, 1))
-        second(0, S, (2, 3))
-        fetch_old(3, "sq2")
-        scatter(0, *pieces[2])
-        finish(0)
-        scatter(1, *pieces[2])
-        finish(1)
-        scatter(2, 0, S)
-        finish(2)
-        scatter(3, 0, S)
-        finish(3)
+        fetch_old(1, "old1")
+        fetch_old(2, "old2")
+        for i in range(2):
+            slope(i, square(i, tanh(i)))
+        z_codes, z_scales = quant(z[:].rearrange("p c t -> p (c t)"), "zq", S)
+        w2_g = deal(w2_raw, "w2_g", 32)
+        w2q = quant(w2_g[:].rearrange("p t m j -> p (t m j)"), "w2q", N)
+        second(0, S, range(PACK))
+        fetch_old(3, "w2_g")
+        for t in range(PACK):
+            scatter(t, 0, S)
+            finish(t)
 
         out_scales = sb("out_scales", [P, U], U8)
         words = out_1[0].rearrange("p c r -> p (c r)").bitcast(I32)
-        for c in range(2):
-            codes = sb(f"out_codes{c}", [P, COLS], U32)
+        for c in (1, 0, 2):
+            lo, hi = chunks[c]
+            codes = sb(f"out_codes{c}", [P, hi - lo], U32)
             nc.vector.quantize_mx(
-                out=codes[:].bitcast(FP8X4),
-                scales=out_scales[:, c * COLS:(c + 1) * COLS],
-                in_=grp[c][:].rearrange("p c t -> p (c t)"),
+                out=codes[:].bitcast(FP8X4), scales=out_scales[:, lo:hi], in_=grp[c][:].rearrange("p c t -> p (c t)")
             )
-            nc.sync.dma_start(words[:, c * COLS:(c + 1) * COLS], codes[:].bitcast(I32))
+            nc.sync.dma_start(words[:, lo:hi], codes[:].bitcast(I32))
         for q in range(4):
             eng = nc.sync if q % 2 == 0 else nc.scalar
             eng.dma_start(out_2[0, 4 * q:4 * q + 4, :].bitcast(I32), out_scales[32 * q:32 * q + 4, :].bitcast(I32))

@@ -43,15 +43,11 @@ def tile_picked_yham_euler_po_kernel(
         bias_sb = sb("bias_sb", [P, PACK], F32)
         top_sb = sb("top_sb", [P, PACK], F32)
         ntop = sb("ntop", [P, PACK], F32)
-        warm_in = sb("warm_in", [P, 1], F32)
-        warm_out = sb("warm_out", [P, 1], F32)
 
         mom_rows = mom.rearrange("(p t) c -> t p c", t=PACK)
         out_rows = out_0.rearrange("(p t) c -> t p c", t=PACK)
 
         nc.vector.memset(xs_win[:].bitcast(I32), 0)
-        nc.vector.memset(warm_in[:], 0.0)
-        nc.scalar.activation(warm_out[:], warm_in[:], ACT.Tanh)
 
         nc.sync.dma_start(offs_sb[:], offs)
         for g in range(PASSES):
@@ -59,18 +55,18 @@ def tile_picked_yham_euler_po_kernel(
             if g == 0:
                 for q in range(4):
                     nc.sync.dma_start(xs_win[32 * q:32 * q + 8, :].bitcast(I32), x_scales[:, 4 * q:4 * q + 4, :].bitcast(I32))
-        for g in range(PASSES):
-            nc.sync.dma_start(xw_win[g][:].bitcast(I32), x_words[g].rearrange("p c r -> p (c r)").bitcast(I32))
         nc.sync.dma_start(bias_sb[:], bias.rearrange("(p t) o -> p (t o)", t=PACK))
         nc.sync.dma_start(top_sb[:], top.rearrange("(p t) o -> p (t o)", t=PACK))
         nc.sync.dma_start(slot_sb[:], slot)
+        for g in range(PASSES):
+            nc.sync.dma_start(xw_win[g][:].bitcast(I32), x_words[g].rearrange("p c r -> p (c r)").bitcast(I32))
         for t in range(PACK):
             nc.sync.dma_start(y[t][:], mom_rows[t])
             if t == 2:
                 nc.sync.dma_start(w2_raw[:], w2.rearrange("(p j) c -> p j c", j=PACK))
 
-        def deal(raw, name, split):
-            grouped = sb(name, [P, PACK, P, PACK], BF16)
+        def deal(raw, name, split, tag=None):
+            grouped = sb(name, [P, PACK, P, PACK], BF16, tag=tag)
             dst = grouped[:].rearrange("p t m j -> p m j t")
             src = raw[:].rearrange("p j (m t) -> p m j t", t=PACK)
             if split > 0:
@@ -148,8 +144,8 @@ def tile_picked_yham_euler_po_kernel(
                 acc = psum.tile([P, hi - lo], F32, name="acc")
                 nc.tensor.matmul_mx(
                     out=acc[:],
-                    lhsT=w2q[0][:, t * P:(t + 1) * P].bitcast(FP8X4),
-                    lhsT_scale=w2q[1][:, t * P:(t + 1) * P],
+                    lhsT=w2q[t // 2][0][:, t % 2 * P:(t % 2 + 1) * P].bitcast(FP8X4),
+                    lhsT_scale=w2q[t // 2][1][:, t % 2 * P:(t % 2 + 1) * P],
                     rhs=z_codes[:, lo:hi].bitcast(FP8X4),
                     rhs_scale=z_scales[:, lo:hi],
                     start=True,
@@ -183,10 +179,10 @@ def tile_picked_yham_euler_po_kernel(
         for i in range(2):
             slope(i, square(i, tanh(i)))
         z_codes, z_scales = quant(z[:].rearrange("p c t -> p (c t)"), "zq", S)
-        w2_g = deal(w2_raw, "w2_g", 32)
-        w2q = quant(w2_g[:].rearrange("p t m j -> p (t m j)"), "w2q", N)
+        w2_g = deal(w2_raw, "w2_g", 32, "h1")
+        w2q = [quant(w2_g[:, 2 * u:2 * u + 2].rearrange("p t m j -> p (t m j)"), f"w2q{u}", 2 * P) for u in range(2)]
         second(0, S, range(PACK))
-        fetch_old(3, "w2_g")
+        fetch_old(3, "h1")
         for t in range(PACK):
             scatter(t, 0, S)
             finish(t)

@@ -42,7 +42,6 @@ def tile_picked_yham_euler_po_kernel(
         y = [sb(f"y{t}", [P, U], F32) for t in range(PACK)]
         bias_sb = sb("bias_sb", [P, PACK], F32)
         top_sb = sb("top_sb", [P, PACK], F32)
-        ntop = sb("ntop", [P, PACK], F32)
 
         mom_rows = mom.rearrange("(p t) c -> t p c", t=PACK)
         out_rows = out_0.rearrange("(p t) c -> t p c", t=PACK)
@@ -52,14 +51,15 @@ def tile_picked_yham_euler_po_kernel(
         nc.sync.dma_start(offs_sb[:], offs)
         for g in range(PASSES):
             nc.sync.dma_start(w1_raw[g][:], w1[g * 512:(g + 1) * 512, :].rearrange("(p j) c -> p j c", j=PACK))
-            if g == 0:
-                for q in range(4):
-                    nc.sync.dma_start(xs_win[32 * q:32 * q + 8, :].bitcast(I32), x_scales[:, 4 * q:4 * q + 4, :].bitcast(I32))
-        nc.sync.dma_start(bias_sb[:], bias.rearrange("(p t) o -> p (t o)", t=PACK))
-        nc.sync.dma_start(top_sb[:], top.rearrange("(p t) o -> p (t o)", t=PACK))
-        nc.sync.dma_start(slot_sb[:], slot)
+            for r in range(2 * g, 2 * g + 2):
+                for k in range(PASSES):
+                    nc.sync.dma_start(xs_win[4 * k + r:P:32, :].bitcast(I32), x_scales[k, r:16:4, :].bitcast(I32))
         for g in range(PASSES):
             nc.sync.dma_start(xw_win[g][:].bitcast(I32), x_words[g].rearrange("p c r -> p (c r)").bitcast(I32))
+            if g == 0:
+                nc.sync.dma_start(bias_sb[:], bias.rearrange("(p t) o -> p (t o)", t=PACK))
+                nc.sync.dma_start(top_sb[:], top.rearrange("(p t) o -> p (t o)", t=PACK))
+                nc.sync.dma_start(slot_sb[:], slot)
         for t in range(PACK):
             nc.sync.dma_start(y[t][:], mom_rows[t])
             if t == 2:
@@ -85,8 +85,7 @@ def tile_picked_yham_euler_po_kernel(
         for g in range(PASSES):
             grouped = deal(w1_raw[g], f"w1_g{g}", 80)
             w1q.append(quant(grouped[:].rearrange("p t m j -> p (t m j)"), f"w1q{g}", H))
-            if g == 0:
-                nc.vector.tensor_copy(xs[:], xs_win[:].indirect(offs_sb[:]))
+        nc.vector.tensor_copy(xs[:], xs_win[:].indirect(offs_sb[:]))
 
         xw = {}
         acc1 = {}
@@ -131,12 +130,21 @@ def tile_picked_yham_euler_po_kernel(
             )
             return sq
 
-        z = sb("z", [P, S, PACK], BF16)
+        z_codes = sb("z_codes", [P, S], U32)
+        z_scales = sb("z_scales", [P, S], U8)
 
         def slope(i, sq):
             lo, hi = pieces[i]
+            z = sb(f"z{i}", [P, hi - lo, PACK], BF16)
             nc.vector.scalar_tensor_tensor(
-                z[:, lo:hi, :], sq[:], 1.0, ntop[:].unsqueeze(1).to_broadcast([P, hi - lo, PACK]), ALU.subtract, ALU.mult
+                z[:], sq[:], 1.0, top_sb[:].unsqueeze(1).to_broadcast([P, hi - lo, PACK]), ALU.subtract, ALU.mult
+            )
+            return z
+
+        def quant_z(i, z):
+            lo, hi = pieces[i]
+            nc.vector.quantize_mx(
+                out=z_codes[:, lo:hi].bitcast(FP8X4), scales=z_scales[:, lo:hi], in_=z[:].rearrange("p c t -> p (c t)")
             )
 
         def second(lo, hi, ts):
@@ -151,7 +159,7 @@ def tile_picked_yham_euler_po_kernel(
                     start=True,
                     stop=True,
                 )
-                nc.scalar.activation(kick[t][:, lo:hi], acc[:], ACT.Copy, scale=-0.2)
+                nc.scalar.activation(kick[t][:, lo:hi], acc[:], ACT.Copy, scale=0.2)
 
         def scatter(t, lo, hi):
             nc.vector.tensor_tensor(
@@ -172,17 +180,23 @@ def tile_picked_yham_euler_po_kernel(
                 else:
                     nc.scalar.copy(grp[c][:, :, t], src)
 
-        nc.scalar.activation(ntop[:], top_sb[:], ACT.Copy, scale=-1.0)
         fetch_old(0, "old0")
         fetch_old(1, "old1")
         fetch_old(2, "old2")
-        for i in range(2):
-            slope(i, square(i, tanh(i)))
-        z_codes, z_scales = quant(z[:].rearrange("p c t -> p (c t)"), "zq", S)
-        w2_g = deal(w2_raw, "w2_g", 32, "h1")
-        w2q = [quant(w2_g[:, 2 * u:2 * u + 2].rearrange("p t m j -> p (t m j)"), f"w2q{u}", 2 * P) for u in range(2)]
-        second(0, S, range(PACK))
-        fetch_old(3, "h1")
+        quant_z(0, slope(0, square(0, tanh(0))))
+        z_last = slope(1, square(1, tanh(1)))
+        w2q = []
+        for u in range(2):
+            w2_g = sb(f"w2_g{u}", [P, 2, P, PACK], BF16, tag=("h1", "sq1")[u])
+            nc.scalar.copy(
+                w2_g[:].rearrange("p t m j -> p m j t"),
+                w2_raw[:].rearrange("p j (m t) -> p m j t", t=PACK)[:, :, :, 2 * u:2 * u + 2],
+            )
+            w2q.append(quant(w2_g[:].rearrange("p t m j -> p (t m j)"), f"w2q{u}", 2 * P))
+            if u == 0:
+                quant_z(1, z_last)
+                fetch_old(3, "h1")
+            second(0, S, range(2 * u, 2 * u + 2))
         for t in range(PACK):
             scatter(t, 0, S)
             finish(t)

@@ -49,19 +49,29 @@ def tile_picked_yham_euler_po_kernel(
         nc.vector.memset(xs_win[:].bitcast(I32), 0)
 
         nc.sync.dma_start(offs_sb[:], offs)
-        for g in range(PASSES):
+        def load_w1(g):
             nc.sync.dma_start(w1_raw[g][:], w1[g * 512:(g + 1) * 512, :].rearrange("(p j) c -> p j c", j=PACK))
-            for r in range(2 * g, 2 * g + 2):
-                for k in range(PASSES):
-                    nc.sync.dma_start(xs_win[4 * k + r:P:32, :].bitcast(I32), x_scales[k, r:16:4, :].bitcast(I32))
-        for g in range(PASSES):
+
+        def load_words(g):
             nc.sync.dma_start(xw_win[g][:].bitcast(I32), x_words[g].rearrange("p c r -> p (c r)").bitcast(I32))
-            if g == 0:
-                nc.sync.dma_start(bias_sb[:], bias.rearrange("(p t) o -> p (t o)", t=PACK))
-                nc.sync.dma_start(top_sb[:], top.rearrange("(p t) o -> p (t o)", t=PACK))
-                nc.sync.dma_start(slot_sb[:], slot)
+
+        def load_scales(rows):
+            for r in rows:
+                for g in range(PASSES):
+                    nc.sync.dma_start(xs_win[4 * g + r:P:32, :].bitcast(I32), x_scales[g, r:16:4, :].bitcast(I32))
+
+        load_w1(0)
+        load_scales((0, 1))
+        load_words(0)
+        load_scales((2, 3))
+        load_w1(1)
+        nc.sync.dma_start(bias_sb[:], bias.rearrange("(p t) o -> p (t o)", t=PACK))
+        nc.sync.dma_start(slot_sb[:], slot)
+        load_words(1)
         for t in range(PACK):
             nc.sync.dma_start(y[t][:], mom_rows[t])
+            if t == 0:
+                nc.sync.dma_start(top_sb[:], top.rearrange("(p t) o -> p (t o)", t=PACK))
             if t == 2:
                 nc.sync.dma_start(w2_raw[:], w2.rearrange("(p j) c -> p j c", j=PACK))
 
@@ -82,14 +92,13 @@ def tile_picked_yham_euler_po_kernel(
 
         w1q = []
         xs = sb("xs", [P, S], U8)
-        for g in range(PASSES):
-            grouped = deal(w1_raw[g], f"w1_g{g}", 80)
-            w1q.append(quant(grouped[:].rearrange("p t m j -> p (t m j)"), f"w1q{g}", H))
-        nc.vector.tensor_copy(xs[:], xs_win[:].indirect(offs_sb[:]))
-
         xw = {}
         acc1 = {}
         for g in range(PASSES):
+            grouped = deal(w1_raw[g], f"w1_g{g}", 80)
+            w1q.append(quant(grouped[:].rearrange("p t m j -> p (t m j)"), f"w1q{g}", H))
+            if g == 0:
+                nc.vector.tensor_copy(xs[:], xs_win[:].indirect(offs_sb[:]))
             for hf in range(2):
                 xw[g, hf] = sb(f"xw{g}{hf}", [P, HALF], U32)
                 nc.vector.tensor_copy(xw[g, hf][:], xw_win[g][:].indirect(offs_sb[:, hf * 16:(hf + 1) * 16]))
@@ -130,8 +139,7 @@ def tile_picked_yham_euler_po_kernel(
             )
             return sq
 
-        z_codes = sb("z_codes", [P, S], U32)
-        z_scales = sb("z_scales", [P, S], U8)
+        zq = {}
 
         def slope(i, sq):
             lo, hi = pieces[i]
@@ -141,25 +149,26 @@ def tile_picked_yham_euler_po_kernel(
             )
             return z
 
-        def quant_z(i, z):
-            lo, hi = pieces[i]
-            nc.vector.quantize_mx(
-                out=z_codes[:, lo:hi].bitcast(FP8X4), scales=z_scales[:, lo:hi], in_=z[:].rearrange("p c t -> p (c t)")
-            )
+        def quant_z(i, z, tag=None):
+            codes = sb(f"z_codes{i}", [P, HALF], U32, tag=tag)
+            scales = sb(f"z_scales{i}", [P, HALF], U8)
+            nc.vector.quantize_mx(out=codes[:].bitcast(FP8X4), scales=scales[:], in_=z[:].rearrange("p c t -> p (c t)"))
+            zq[i] = codes, scales
 
-        def second(lo, hi, ts):
+        def second(ts):
             for t in ts:
-                acc = psum.tile([P, hi - lo], F32, name="acc")
-                nc.tensor.matmul_mx(
-                    out=acc[:],
-                    lhsT=w2q[t // 2][0][:, t % 2 * P:(t % 2 + 1) * P].bitcast(FP8X4),
-                    lhsT_scale=w2q[t // 2][1][:, t % 2 * P:(t % 2 + 1) * P],
-                    rhs=z_codes[:, lo:hi].bitcast(FP8X4),
-                    rhs_scale=z_scales[:, lo:hi],
-                    start=True,
-                    stop=True,
-                )
-                nc.scalar.activation(kick[t][:, lo:hi], acc[:], ACT.Copy, scale=0.2)
+                acc = psum.tile([P, S], F32, name="acc")
+                for i, (lo, hi) in enumerate(pieces):
+                    nc.tensor.matmul_mx(
+                        out=acc[:, lo:hi],
+                        lhsT=w2q[t // 2][0][:, t % 2 * P:(t % 2 + 1) * P].bitcast(FP8X4),
+                        lhsT_scale=w2q[t // 2][1][:, t % 2 * P:(t % 2 + 1) * P],
+                        rhs=zq[i][0][:].bitcast(FP8X4),
+                        rhs_scale=zq[i][1][:],
+                        start=True,
+                        stop=True,
+                    )
+                nc.scalar.activation(kick[t][:], acc[:], ACT.Copy, scale=0.2)
 
         def scatter(t, lo, hi):
             nc.vector.tensor_tensor(
@@ -194,9 +203,9 @@ def tile_picked_yham_euler_po_kernel(
             )
             w2q.append(quant(w2_g[:].rearrange("p t m j -> p (t m j)"), f"w2q{u}", 2 * P))
             if u == 0:
-                quant_z(1, z_last)
-                fetch_old(3, "h1")
-            second(0, S, range(2 * u, 2 * u + 2))
+                quant_z(1, z_last, "h1")
+                fetch_old(3, "z1")
+            second(range(2 * u, 2 * u + 2))
         for t in range(PACK):
             scatter(t, 0, S)
             finish(t)
@@ -210,6 +219,6 @@ def tile_picked_yham_euler_po_kernel(
                 out=codes[:].bitcast(FP8X4), scales=out_scales[:, lo:hi], in_=grp[c][:].rearrange("p c t -> p (c t)")
             )
             nc.sync.dma_start(words[:, lo:hi], codes[:].bitcast(I32))
-        for q in range(4):
-            eng = nc.sync if q % 2 == 0 else nc.scalar
-            eng.dma_start(out_2[0, 4 * q:4 * q + 4, :].bitcast(I32), out_scales[32 * q:32 * q + 4, :].bitcast(I32))
+        for r in range(4):
+            eng = nc.sync if r % 2 == 0 else nc.scalar
+            eng.dma_start(out_2[0, r:16:4, :].bitcast(I32), out_scales[r:P:32, :].bitcast(I32))

@@ -20,6 +20,7 @@ PACK = 4
 PASSES = K // (P * PACK)
 HALF = S // 2
 COLS = U // 2
+QUARTER = U // 4
 
 
 def tile_picked_yham_euler_po_kernel(
@@ -48,7 +49,6 @@ def tile_picked_yham_euler_po_kernel(
 
         nc.vector.memset(xs_win[:].bitcast(I32), 0)
 
-        nc.sync.dma_start(offs_sb[:], offs)
         def load_w1(g):
             nc.sync.dma_start(w1_raw[g][:], w1[g * 512:(g + 1) * 512, :].rearrange("(p j) c -> p j c", j=PACK))
 
@@ -61,6 +61,7 @@ def tile_picked_yham_euler_po_kernel(
                     nc.sync.dma_start(xs_win[4 * g + r:P:32, :].bitcast(I32), x_scales[g, r:16:4, :].bitcast(I32))
 
         load_w1(0)
+        nc.sync.dma_start(offs_sb[:], offs)
         load_scales((0, 1))
         load_words(0)
         load_scales((2, 3))
@@ -175,19 +176,20 @@ def tile_picked_yham_euler_po_kernel(
                 y[t][:].indirect(slot_sb[:, lo // 16:hi // 16]), old[t][:, lo:hi], kick[t][:, lo:hi], ALU.add
             )
 
-        chunks = [(0, 512), (512, 768), (768, 1024)]
-        grp = [sb(f"grp{c}", [P, hi - lo, PACK], BF16) for c, (lo, hi) in enumerate(chunks)]
+        grp = [sb(f"grp{c}", [P, COLS, PACK], BF16) for c in range(2)]
 
         def finish(t):
             nc.sync.dma_start(out_rows[t], y[t][:])
-            for c, (lo, hi) in enumerate(chunks):
-                src = y[t][:, lo:hi]
-                if t == PACK - 1 and c == 0:
-                    nc.vector.tensor_copy(grp[c][:, :, t], src)
-                elif t == PACK - 2 and c == 0:
-                    nc.scalar.copy(grp[c][:, :, t:t + 2], src.unsqueeze(2).to_broadcast([P, hi - lo, 2]))
-                else:
-                    nc.scalar.copy(grp[c][:, :, t], src)
+            if t == PACK - 1:
+                nc.vector.tensor_copy(grp[0][:, :, t], y[t][:, :COLS])
+                for lo in (0, QUARTER):
+                    nc.scalar.copy(grp[1][:, lo:lo + QUARTER, t], y[t][:, COLS + lo:COLS + lo + QUARTER])
+                return
+            if t == PACK - 2:
+                nc.scalar.copy(grp[0][:, :, t:t + 2], y[t][:, :COLS].unsqueeze(2).to_broadcast([P, COLS, 2]))
+            else:
+                nc.scalar.copy(grp[0][:, :, t], y[t][:, :COLS])
+            nc.scalar.copy(grp[1][:, :, t], y[t][:, COLS:])
 
         fetch_old(0, "old0")
         fetch_old(1, "old1")
@@ -212,11 +214,11 @@ def tile_picked_yham_euler_po_kernel(
 
         out_scales = sb("out_scales", [P, U], U8)
         words = out_1[0].rearrange("p c r -> p (c r)").bitcast(I32)
-        for c in (1, 0, 2):
-            lo, hi = chunks[c]
-            codes = sb(f"out_codes{c}", [P, hi - lo], U32)
+        for lo, hi in ((512, 768), (0, 512), (768, 1024)):
+            codes = sb(f"out_codes{lo}", [P, hi - lo], U32)
+            src = grp[lo // COLS][:, lo % COLS:lo % COLS + hi - lo]
             nc.vector.quantize_mx(
-                out=codes[:].bitcast(FP8X4), scales=out_scales[:, lo:hi], in_=grp[c][:].rearrange("p c t -> p (c t)")
+                out=codes[:].bitcast(FP8X4), scales=out_scales[:, lo:hi], in_=src.rearrange("p c t -> p (c t)")
             )
             nc.sync.dma_start(words[:, lo:hi], codes[:].bitcast(I32))
         for r in range(4):

@@ -21,6 +21,7 @@ PASSES = K // (P * PACK)
 HALF = S // 2
 COLS = U // 2
 QUARTER = U // 4
+LATE = 64
 
 
 def tile_picked_yham_euler_po_kernel(
@@ -69,11 +70,11 @@ def tile_picked_yham_euler_po_kernel(
         nc.sync.dma_start(bias_sb[:], bias.rearrange("(p t) o -> p (t o)", t=PACK))
         nc.sync.dma_start(slot_sb[:], slot)
         load_words(1)
-        for t in range(PACK):
+        for t in (0, 2, 3, 1):
             nc.sync.dma_start(y[t][:], mom_rows[t])
             if t == 0:
                 nc.sync.dma_start(top_sb[:], top.rearrange("(p t) o -> p (t o)", t=PACK))
-            if t == 2:
+            if t == 3:
                 nc.sync.dma_start(w2_raw[:], w2.rearrange("(p j) c -> p j c", j=PACK))
 
         def deal(raw, name, split, tag=None):
@@ -118,11 +119,15 @@ def tile_picked_yham_euler_po_kernel(
 
         pieces = [(0, HALF), (HALF, S)]
         old = {}
-        kick = [sb(f"kick{t}", [P, S], F32) for t in range(PACK)]
+        order = (0, 2, 3, 1)
+        last = order[-1]
+        shared = sb("shared", [P, 2 * S - LATE], F32)
+        kick = {t: sb(f"kick{t}", [P, S], F32)[:] for t in order[:-1]}
+        kick[last] = shared[:, S - LATE:]
 
         def fetch_old(t, tag):
-            old[t] = sb(f"old{t}", [P, S], F32, tag=tag)
-            nc.vector.tensor_copy(old[t][:], y[t][:].indirect(slot_sb[:]))
+            old[t] = shared[:, :S] if t == order[0] else sb(f"old{t}", [P, S], F32, tag=tag)[:]
+            nc.vector.tensor_copy(old[t], y[t][:].indirect(slot_sb[:]))
 
         def tanh(i):
             lo, hi = pieces[i]
@@ -156,9 +161,15 @@ def tile_picked_yham_euler_po_kernel(
             nc.vector.quantize_mx(out=codes[:].bitcast(FP8X4), scales=scales[:], in_=z[:].rearrange("p c t -> p (c t)"))
             zq[i] = codes, scales
 
+        acc2 = {}
+
+        def scale_out(t, lo, hi):
+            nc.scalar.activation(kick[t][:, lo:hi], acc2[t][:, lo:hi], ACT.Copy, scale=0.2)
+
         def second(ts):
             for t in ts:
                 acc = psum.tile([P, S], F32, name="acc")
+                acc2[t] = acc
                 for i, (lo, hi) in enumerate(pieces):
                     nc.tensor.matmul_mx(
                         out=acc[:, lo:hi],
@@ -169,31 +180,27 @@ def tile_picked_yham_euler_po_kernel(
                         start=True,
                         stop=True,
                     )
-                nc.scalar.activation(kick[t][:], acc[:], ACT.Copy, scale=0.2)
+                scale_out(t, LATE if t == last else 0, S)
 
         def scatter(t, lo, hi):
             nc.vector.tensor_tensor(
                 y[t][:].indirect(slot_sb[:, lo // 16:hi // 16]), old[t][:, lo:hi], kick[t][:, lo:hi], ALU.add
             )
 
-        grp = [sb(f"grp{c}", [P, COLS, PACK], BF16) for c in range(2)]
+        chunks = [(0, 512), (512, 768), (768, 1024)]
+        grp = [sb(f"grp{c}", [P, hi - lo, PACK], BF16) for c, (lo, hi) in enumerate(chunks)]
 
         def finish(t):
             nc.sync.dma_start(out_rows[t], y[t][:])
-            if t == PACK - 1:
-                nc.vector.tensor_copy(grp[0][:, :, t], y[t][:, :COLS])
-                for lo in (0, QUARTER):
-                    nc.scalar.copy(grp[1][:, lo:lo + QUARTER, t], y[t][:, COLS + lo:COLS + lo + QUARTER])
-                return
-            if t == PACK - 2:
-                nc.scalar.copy(grp[0][:, :, t:t + 2], y[t][:, :COLS].unsqueeze(2).to_broadcast([P, COLS, 2]))
-            else:
-                nc.scalar.copy(grp[0][:, :, t], y[t][:, :COLS])
-            nc.scalar.copy(grp[1][:, :, t], y[t][:, COLS:])
+            for c, (lo, hi) in enumerate(chunks):
+                copy = nc.vector.tensor_copy if t == last and c == 0 else nc.scalar.copy
+                copy(grp[c][:, :, t], y[t][:, lo:hi])
+                if t == order[0] and c == 0:
+                    scale_out(last, 0, LATE)
 
         fetch_old(0, "old0")
-        fetch_old(1, "old1")
         fetch_old(2, "old2")
+        fetch_old(3, "old3")
         quant_z(0, slope(0, square(0, tanh(0))))
         z_last = slope(1, square(1, tanh(1)))
         w2q = []
@@ -206,17 +213,18 @@ def tile_picked_yham_euler_po_kernel(
             w2q.append(quant(w2_g[:].rearrange("p t m j -> p (t m j)"), f"w2q{u}", 2 * P))
             if u == 0:
                 quant_z(1, z_last, "h1")
-                fetch_old(3, "z1")
+                fetch_old(1, "z1")
             second(range(2 * u, 2 * u + 2))
-        for t in range(PACK):
+        for t in order:
             scatter(t, 0, S)
             finish(t)
 
         out_scales = sb("out_scales", [P, U], U8)
         words = out_1[0].rearrange("p c r -> p (c r)").bitcast(I32)
-        for lo, hi in ((512, 768), (0, 512), (768, 1024)):
-            codes = sb(f"out_codes{lo}", [P, hi - lo], U32)
-            src = grp[lo // COLS][:, lo % COLS:lo % COLS + hi - lo]
+        for c, tag in ((1, None), (0, "grp1"), (2, "grp0")):
+            lo, hi = chunks[c]
+            codes = sb(f"out_codes{c}", [P, hi - lo], U32, tag=tag)
+            src = grp[c][:]
             nc.vector.quantize_mx(
                 out=codes[:].bitcast(FP8X4), scales=out_scales[:, lo:hi], in_=src.rearrange("p c t -> p (c t)")
             )

@@ -187,16 +187,23 @@ def tile_picked_yham_euler_po_kernel(
                 y[t][:].indirect(slot_sb[:, lo // 16:hi // 16]), old[t][:, lo:hi], kick[t][:, lo:hi], ALU.add
             )
 
-        chunks = [(0, 512), (512, 768), (768, 1024)]
-        grp = [sb(f"grp{c}", [P, hi - lo, PACK], BF16) for c, (lo, hi) in enumerate(chunks)]
+        grp = [sb(f"grp{c}", [P, COLS, PACK], BF16) for c in range(2)]
+
+        def round_plane(copy, t, lo, hi):
+            first = lo // COLS * COLS
+            copy(grp[lo // COLS][:, lo - first:hi - first, t], y[t][:, lo:hi])
 
         def finish(t):
             nc.sync.dma_start(out_rows[t], y[t][:])
-            for c, (lo, hi) in enumerate(chunks):
-                copy = nc.vector.tensor_copy if t == last and c == 0 else nc.scalar.copy
-                copy(grp[c][:, :, t], y[t][:, lo:hi])
-                if t == order[0] and c == 0:
-                    scale_out(last, 0, LATE)
+            if t == last:
+                for lo in (0, COLS):
+                    round_plane(nc.vector.tensor_copy, t, lo, lo + QUARTER)
+                    round_plane(nc.scalar.copy, t, lo + QUARTER, lo + COLS)
+                return
+            for lo in (0, COLS):
+                round_plane(nc.scalar.copy, t, lo, lo + COLS)
+            if t == order[0]:
+                scale_out(last, 0, LATE)
 
         fetch_old(0, "old0")
         fetch_old(2, "old2")
@@ -221,14 +228,17 @@ def tile_picked_yham_euler_po_kernel(
 
         out_scales = sb("out_scales", [P, U], U8)
         words = out_1[0].rearrange("p c r -> p (c r)").bitcast(I32)
-        for c, tag in ((1, None), (0, "grp1"), (2, "grp0")):
-            lo, hi = chunks[c]
-            codes = sb(f"out_codes{c}", [P, hi - lo], U32, tag=tag)
-            src = grp[c][:]
+        codes = sb("out_codes", [P, U], U32)
+        stored = 0
+        for c in range(4):
+            lo, hi = c * QUARTER, (c + 1) * QUARTER
+            src = grp[c // 2][:, c % 2 * QUARTER:(c % 2 + 1) * QUARTER]
             nc.vector.quantize_mx(
-                out=codes[:].bitcast(FP8X4), scales=out_scales[:, lo:hi], in_=src.rearrange("p c t -> p (c t)")
+                out=codes[:, lo:hi].bitcast(FP8X4), scales=out_scales[:, lo:hi], in_=src.rearrange("p c t -> p (c t)")
             )
-            nc.sync.dma_start(words[:, lo:hi], codes[:].bitcast(I32))
+            if c > 0:
+                nc.sync.dma_start(words[:, stored:hi], codes[:, stored:hi].bitcast(I32))
+                stored = hi
         for r in range(4):
             eng = nc.sync if r % 2 == 0 else nc.scalar
             eng.dma_start(out_2[0, r:16:4, :].bitcast(I32), out_scales[r:P:32, :].bitcast(I32))

@@ -72,9 +72,8 @@ def tile_picked_yham_euler_po_kernel(
         load_words(1)
         for t in (0, 2, 3, 1):
             nc.sync.dma_start(y[t][:], mom_rows[t])
-            if t == 0:
-                nc.sync.dma_start(top_sb[:], top.rearrange("(p t) o -> p (t o)", t=PACK))
             if t == 3:
+                nc.sync.dma_start(top_sb[:], top.rearrange("(p t) o -> p (t o)", t=PACK))
                 nc.sync.dma_start(w2_raw[:], w2.rearrange("(p j) c -> p j c", j=PACK))
 
         def deal(raw, name, split, tag=None):
@@ -168,6 +167,20 @@ def tile_picked_yham_euler_po_kernel(
 
         def second(ts):
             for t in ts:
+                if t == order[0]:
+                    for i, (lo, hi) in enumerate(pieces):
+                        part = psum.tile([P, HALF], F32, name="acc")
+                        nc.tensor.matmul_mx(
+                            out=part[:],
+                            lhsT=w2q[t // 2][0][:, t % 2 * P:(t % 2 + 1) * P].bitcast(FP8X4),
+                            lhsT_scale=w2q[t // 2][1][:, t % 2 * P:(t % 2 + 1) * P],
+                            rhs=zq[i][0][:].bitcast(FP8X4),
+                            rhs_scale=zq[i][1][:],
+                            start=True,
+                            stop=True,
+                        )
+                        nc.scalar.activation(kick[t][:, lo:hi], part[:], ACT.Copy, scale=0.2)
+                    continue
                 acc = psum.tile([P, S], F32, name="acc")
                 acc2[t] = acc
                 for i, (lo, hi) in enumerate(pieces):

@@ -32,7 +32,12 @@ def tile_picked_yham_euler_po_kernel(
         keep = ctx.enter_context(tc.tile_pool(name="keep", bufs=1))
         psum = ctx.enter_context(tc.psum_pool(name="psum", bufs=8))
 
+        held = ctx.enter_context(tc.tile_pool(name="held", bufs=1))
+        places = {"h": 0, "w2_g0": 0, "w2_g1": 2048, "z_codes0": 4096, "w2_raw": 8192, "old1": 8192}
+
         def sb(name, shape, dtype, tag=None):
+            if name in places:
+                return held.tile(shape, dtype, name=name, tag=name, align_bytes=64, offset=places[name])
             return keep.tile(shape, dtype, name=name, tag=tag or name, align_bytes=64)
 
         offs_sb = keep.tile([P, S // 16], U16, name="offs_sb")
@@ -128,9 +133,11 @@ def tile_picked_yham_euler_po_kernel(
             old[t] = shared[:, :S] if t == order[0] else sb(f"old{t}", [P, S], F32, tag=tag)[:]
             nc.vector.tensor_copy(old[t], y[t][:].indirect(slot_sb[:]))
 
+        h_all = sb("h", [P, 2, PACK, HALF], F32)
+
         def tanh(i):
             lo, hi = pieces[i]
-            h = sb(f"h{i}", [P, PACK, hi - lo], F32)
+            h = h_all[:, i]
             for t in range(PACK):
                 src = acc1[lo // HALF, t][:, lo % HALF:lo % HALF + hi - lo]
                 nc.scalar.activation(h[:, t, :], src, ACT.Tanh, bias=bias_sb[:, t:t + 1])
@@ -140,7 +147,7 @@ def tile_picked_yham_euler_po_kernel(
             lo, hi = pieces[i]
             sq = sb(f"sq{i}", [P, hi - lo, PACK], F32)
             nc.scalar.activation(
-                sq[:].rearrange("p (c i) t -> p c t i", i=4), h[:].rearrange("p t (c i) -> p c t i", i=4), ACT.Square
+                sq[:].rearrange("p (c i) t -> p c t i", i=4), h.rearrange("p t (c i) -> p c t i", i=4), ACT.Square
             )
             return sq
 
@@ -221,20 +228,20 @@ def tile_picked_yham_euler_po_kernel(
         fetch_old(0, "old0")
         fetch_old(2, "old2")
         fetch_old(3, "old3")
-        quant_z(0, slope(0, square(0, tanh(0))))
+        z_first = slope(0, square(0, tanh(0)))
         z_last = slope(1, square(1, tanh(1)))
+        quant_z(0, z_first)
+        quant_z(1, z_last)
         w2q = []
         for u in range(2):
-            w2_g = sb(f"w2_g{u}", [P, 2, P, PACK], BF16, tag=("h1", "sq1")[u])
+            w2_g = sb(f"w2_g{u}", [P, 2, P, PACK], BF16)
             nc.scalar.copy(
                 w2_g[:].rearrange("p t m j -> p m j t"),
                 w2_raw[:].rearrange("p j (m t) -> p m j t", t=PACK)[:, :, :, 2 * u:2 * u + 2],
             )
             w2q.append(quant(w2_g[:].rearrange("p t m j -> p (t m j)"), f"w2q{u}", 2 * P))
-            if u == 0:
-                quant_z(1, z_last, "h1")
-                fetch_old(1, "z1")
             second(range(2 * u, 2 * u + 2))
+        fetch_old(1, None)
         for t in order:
             scatter(t, 0, S)
             finish(t)

@@ -33,7 +33,7 @@ def tile_picked_yham_euler_po_kernel(
         psum = ctx.enter_context(tc.psum_pool(name="psum", bufs=8))
 
         held = ctx.enter_context(tc.tile_pool(name="held", bufs=1))
-        places = {"h": 0, "w2_g0": 0, "w2_g1": 2048, "z_codes0": 4096, "w2_raw": 8192, "old1": 8192}
+        places = {"h": 0, "w2_g0": 0, "w2_g1": 2048, "z_codes0": 4096, "old1": 0}
 
         def sb(name, shape, dtype, tag=None):
             if name in places:
@@ -72,9 +72,9 @@ def tile_picked_yham_euler_po_kernel(
         load_words(0)
         load_scales((2, 3))
         load_w1(1)
+        load_words(1)
         nc.sync.dma_start(bias_sb[:], bias.rearrange("(p t) o -> p (t o)", t=PACK))
         nc.sync.dma_start(slot_sb[:], slot)
-        load_words(1)
         for t in (0, 2, 3, 1):
             nc.sync.dma_start(y[t][:], mom_rows[t])
             if t == 3:
@@ -240,8 +240,9 @@ def tile_picked_yham_euler_po_kernel(
                 w2_raw[:].rearrange("p j (m t) -> p m j t", t=PACK)[:, :, :, 2 * u:2 * u + 2],
             )
             w2q.append(quant(w2_g[:].rearrange("p t m j -> p (t m j)"), f"w2q{u}", 2 * P))
+            if u == 0:
+                fetch_old(1, None)
             second(range(2 * u, 2 * u + 2))
-        fetch_old(1, None)
         for t in order:
             scatter(t, 0, S)
             finish(t)

@@ -21,7 +21,6 @@ PASSES = K // (P * PACK)
 HALF = S // 2
 COLS = U // 2
 QUARTER = U // 4
-LATE = 64
 
 
 def tile_picked_yham_euler_po_kernel(
@@ -32,12 +31,7 @@ def tile_picked_yham_euler_po_kernel(
         keep = ctx.enter_context(tc.tile_pool(name="keep", bufs=1))
         psum = ctx.enter_context(tc.psum_pool(name="psum", bufs=8))
 
-        held = ctx.enter_context(tc.tile_pool(name="held", bufs=1))
-        places = {"h": 0, "w2_g0": 0, "w2_g1": 2048, "z_codes0": 4096, "old1": 0}
-
         def sb(name, shape, dtype, tag=None):
-            if name in places:
-                return held.tile(shape, dtype, name=name, tag=name, align_bytes=64, offset=places[name])
             return keep.tile(shape, dtype, name=name, tag=tag or name, align_bytes=64)
 
         offs_sb = keep.tile([P, S // 16], U16, name="offs_sb")
@@ -73,13 +67,13 @@ def tile_picked_yham_euler_po_kernel(
         load_scales((2, 3))
         load_w1(1)
         load_words(1)
-        nc.sync.dma_start(bias_sb[:], bias.rearrange("(p t) o -> p (t o)", t=PACK))
         nc.sync.dma_start(slot_sb[:], slot)
-        for t in (0, 2, 3, 1):
+        nc.sync.dma_start(y[0][:], mom_rows[0])
+        nc.sync.dma_start(bias_sb[:], bias.rearrange("(p t) o -> p (t o)", t=PACK))
+        nc.sync.dma_start(w2_raw[:], w2.rearrange("(p j) c -> p j c", j=PACK))
+        nc.sync.dma_start(top_sb[:], top.rearrange("(p t) o -> p (t o)", t=PACK))
+        for t in (1, 3, 2):
             nc.sync.dma_start(y[t][:], mom_rows[t])
-            if t == 3:
-                nc.sync.dma_start(top_sb[:], top.rearrange("(p t) o -> p (t o)", t=PACK))
-                nc.sync.dma_start(w2_raw[:], w2.rearrange("(p j) c -> p j c", j=PACK))
 
         def deal(raw, name, split, tag=None):
             grouped = sb(name, [P, PACK, P, PACK], BF16, tag=tag)
@@ -122,144 +116,137 @@ def tile_picked_yham_euler_po_kernel(
                     )
 
         pieces = [(0, HALF), (HALF, S)]
-        old = {}
-        order = (0, 2, 3, 1)
-        last = order[-1]
-        shared = sb("shared", [P, 2 * S - LATE], F32)
-        kick = {t: sb(f"kick{t}", [P, S], F32)[:] for t in order[:-1]}
-        kick[last] = shared[:, S - LATE:]
+        old = [sb(f"old{t}", [P, S], F32) for t in range(PACK)]
+        new = [sb(f"new{t}", [P, S], F32) for t in range(PACK)]
 
-        def fetch_old(t, tag):
-            old[t] = shared[:, :S] if t == order[0] else sb(f"old{t}", [P, S], F32, tag=tag)[:]
-            nc.vector.tensor_copy(old[t], y[t][:].indirect(slot_sb[:]))
+        def fetch_vector(t):
+            nc.vector.tensor_copy(old[t][:], y[t][:].indirect(slot_sb[:]))
 
-        h_all = sb("h", [P, 2, PACK, HALF], F32)
+        def fetch_scalar(t):
+            nc.scalar.activation(old[t][:], y[t][:].indirect(slot_sb[:]), ACT.Copy)
 
-        def tanh(i):
-            lo, hi = pieces[i]
-            h = h_all[:, i]
+        def tanh_square(i):
+            h = sb(f"h{i}", [P, PACK, HALF], F32)
             for t in range(PACK):
-                src = acc1[lo // HALF, t][:, lo % HALF:lo % HALF + hi - lo]
-                nc.scalar.activation(h[:, t, :], src, ACT.Tanh, bias=bias_sb[:, t:t + 1])
-            return h
-
-        def square(i, h):
-            lo, hi = pieces[i]
-            sq = sb(f"sq{i}", [P, hi - lo, PACK], F32)
-            nc.scalar.activation(
-                sq[:].rearrange("p (c i) t -> p c t i", i=4), h.rearrange("p t (c i) -> p c t i", i=4), ACT.Square
-            )
+                nc.scalar.activation(h[:, t, :], acc1[i, t][:], ACT.Tanh, bias=bias_sb[:, t:t + 1])
+            sq = sb(f"sq{i}", [P, HALF, PACK], F32)
+            dst = sq[:].rearrange("p (c i) t -> p c t i", i=4)
+            src = h[:].rearrange("p t (c i) -> p c t i", i=4)
+            if i == 0:
+                nc.vector.tensor_tensor(dst, src, src, ALU.mult)
+            else:
+                nc.scalar.activation(dst, src, ACT.Square)
             return sq
 
-        zq = {}
-
         def slope(i, sq):
-            lo, hi = pieces[i]
-            z = sb(f"z{i}", [P, hi - lo, PACK], BF16)
+            z = sb(f"z{i}", [P, HALF, PACK], BF16)
             nc.vector.scalar_tensor_tensor(
-                z[:], sq[:], 1.0, top_sb[:].unsqueeze(1).to_broadcast([P, hi - lo, PACK]), ALU.subtract, ALU.mult
+                z[:], sq[:], 1.0, top_sb[:].unsqueeze(1).to_broadcast([P, HALF, PACK]), ALU.subtract, ALU.mult
             )
             return z
 
-        def quant_z(i, z, tag=None):
-            codes = sb(f"z_codes{i}", [P, HALF], U32, tag=tag)
-            scales = sb(f"z_scales{i}", [P, HALF], U8)
-            nc.vector.quantize_mx(out=codes[:].bitcast(FP8X4), scales=scales[:], in_=z[:].rearrange("p c t -> p (c t)"))
-            zq[i] = codes, scales
-
         acc2 = {}
 
-        def scale_out(t, lo, hi):
-            nc.scalar.activation(kick[t][:, lo:hi], acc2[t][:, lo:hi], ACT.Copy, scale=0.2)
+        def second(t, i):
+            acc2[t, i] = psum.tile([P, HALF], F32, name="acc")
+            nc.tensor.matmul_mx(
+                out=acc2[t, i][:],
+                lhsT=w2q[t // 2][0][:, t % 2 * P:(t % 2 + 1) * P].bitcast(FP8X4),
+                lhsT_scale=w2q[t // 2][1][:, t % 2 * P:(t % 2 + 1) * P],
+                rhs=zq[i][0][:].bitcast(FP8X4),
+                rhs_scale=zq[i][1][:],
+                start=True,
+                stop=True,
+            )
 
-        def second(ts):
-            for t in ts:
-                if t == order[0]:
-                    for i, (lo, hi) in enumerate(pieces):
-                        part = psum.tile([P, HALF], F32, name="acc")
-                        nc.tensor.matmul_mx(
-                            out=part[:],
-                            lhsT=w2q[t // 2][0][:, t % 2 * P:(t % 2 + 1) * P].bitcast(FP8X4),
-                            lhsT_scale=w2q[t // 2][1][:, t % 2 * P:(t % 2 + 1) * P],
-                            rhs=zq[i][0][:].bitcast(FP8X4),
-                            rhs_scale=zq[i][1][:],
-                            start=True,
-                            stop=True,
-                        )
-                        nc.scalar.activation(kick[t][:, lo:hi], part[:], ACT.Copy, scale=0.2)
-                    continue
-                acc = psum.tile([P, S], F32, name="acc")
-                acc2[t] = acc
-                for i, (lo, hi) in enumerate(pieces):
-                    nc.tensor.matmul_mx(
-                        out=acc[:, lo:hi],
-                        lhsT=w2q[t // 2][0][:, t % 2 * P:(t % 2 + 1) * P].bitcast(FP8X4),
-                        lhsT_scale=w2q[t // 2][1][:, t % 2 * P:(t % 2 + 1) * P],
-                        rhs=zq[i][0][:].bitcast(FP8X4),
-                        rhs_scale=zq[i][1][:],
-                        start=True,
-                        stop=True,
-                    )
-                scale_out(t, LATE if t == last else 0, S)
+        def kick_out(t, i):
+            lo, hi = pieces[i]
+            nc.scalar.activation(new[t][:, lo:hi], acc2[t, i][:], ACT.Copy, scale=0.2)
 
-        def scatter(t, lo, hi):
+        def kick_add(t, i):
+            lo, hi = pieces[i]
+            nc.vector.scalar_tensor_tensor(new[t][:, lo:hi], acc2[t, i][:], 0.2, old[t][:, lo:hi], ALU.mult, ALU.add)
+
+        def put_vector(t, i):
+            lo, hi = pieces[i]
             nc.vector.tensor_tensor(
-                y[t][:].indirect(slot_sb[:, lo // 16:hi // 16]), old[t][:, lo:hi], kick[t][:, lo:hi], ALU.add
+                y[t][:].indirect(slot_sb[:, lo // 16:hi // 16]), old[t][:, lo:hi], new[t][:, lo:hi], ALU.add
             )
 
-        grp = [sb(f"grp{c}", [P, COLS, PACK], BF16) for c in range(2)]
+        def put_scalar(t, i):
+            lo, hi = pieces[i]
+            nc.scalar.activation(y[t][:].indirect(slot_sb[:, lo // 16:hi // 16]), new[t][:, lo:hi], ACT.Copy)
 
-        def round_plane(copy, t, lo, hi):
-            first = lo // COLS * COLS
-            copy(grp[lo // COLS][:, lo - first:hi - first, t], y[t][:, lo:hi])
-
-        def finish(t):
+        def store(t):
             nc.sync.dma_start(out_rows[t], y[t][:])
-            if t == last:
-                for lo in (0, COLS):
-                    round_plane(nc.vector.tensor_copy, t, lo, lo + QUARTER)
-                    round_plane(nc.scalar.copy, t, lo + QUARTER, lo + COLS)
-                return
-            for lo in (0, COLS):
-                round_plane(nc.scalar.copy, t, lo, lo + COLS)
-            if t == order[0]:
-                scale_out(last, 0, LATE)
 
-        fetch_old(0, "old0")
-        fetch_old(2, "old2")
-        fetch_old(3, "old3")
-        z_first = slope(0, square(0, tanh(0)))
-        z_last = slope(1, square(1, tanh(1)))
-        quant_z(0, z_first)
-        quant_z(1, z_last)
-        w2q = []
-        for u in range(2):
-            w2_g = sb(f"w2_g{u}", [P, 2, P, PACK], BF16)
-            nc.scalar.copy(
-                w2_g[:].rearrange("p t m j -> p m j t"),
-                w2_raw[:].rearrange("p j (m t) -> p m j t", t=PACK)[:, :, :, 2 * u:2 * u + 2],
-            )
-            w2q.append(quant(w2_g[:].rearrange("p t m j -> p (t m j)"), f"w2q{u}", 2 * P))
-            if u == 0:
-                fetch_old(1, None)
-            second(range(2 * u, 2 * u + 2))
-        for t in order:
-            scatter(t, 0, S)
-            finish(t)
+        pairs = [sb(f"pairs{c}", [P, 2, COLS, 2], BF16) for c in range(2)]
+
+        def round_plane(t):
+            for c in range(2):
+                nc.vector.tensor_copy(pairs[c][:, t // 2, :, t % 2], y[t][:, c * COLS:(c + 1) * COLS])
+
+        fetch_vector(0)
+        sq = [tanh_square(i) for i in range(2)]
+        fetch_scalar(1)
+        fetch_scalar(3)
+        zq = {}
+        w2_g = sb("w2_g", [P, PACK, P, PACK], BF16)
+        nc.vector.tensor_copy(w2_g[:].rearrange("p t m j -> p m j t"), w2_raw[:].rearrange("p j (m t) -> p m j t", t=PACK))
+        z_first = slope(0, sq[0])
+        w2q = [quant(w2_g[:, 0:2].rearrange("p t m j -> p (t m j)"), "w2q0", 2 * P)]
+        zq[0] = quant(z_first[:].rearrange("p c t -> p (c t)"), "zq0", HALF)
+        second(1, 0)
+        second(0, 0)
+        w2q.append(quant(w2_g[:, 2:4].rearrange("p t m j -> p (t m j)"), "w2q1", 2 * P))
+        second(3, 0)
+        second(2, 0)
+        kick_add(1, 0)
+        kick_out(0, 0)
+        put_scalar(1, 0)
+        fetch_scalar(2)
+        z_last = slope(1, sq[1])
+        kick_add(3, 0)
+        zq[1] = quant(z_last[:].rearrange("p c t -> p (c t)"), "zq1", HALF)
+        for t in (0, 1, 2, 3):
+            second(t, 1)
+        put_vector(0, 0)
+        kick_out(0, 1)
+        kick_out(2, 0)
+        kick_add(1, 1)
+        kick_add(2, 1)
+        put_scalar(1, 1)
+        store(1)
+        put_scalar(2, 1)
+        put_vector(0, 1)
+        store(0)
+        kick_add(3, 1)
+        put_scalar(3, 0)
+        put_scalar(3, 1)
+        round_plane(0)
+        round_plane(1)
+        put_vector(2, 0)
+        store(2)
+        store(3)
+        round_plane(2)
+        round_plane(3)
 
         out_scales = sb("out_scales", [P, U], U8)
         words = out_1[0].rearrange("p c r -> p (c r)").bitcast(I32)
         codes = sb("out_codes", [P, U], U32)
-        stored = 0
-        for c in range(4):
+        grp = [sb(f"grp{c}", [P, QUARTER * PACK], BF16) for c in range(4)]
+
+        def weave(c, copy, dtype):
+            src = pairs[c // 2][:].rearrange("p u c e -> p u (c e)").bitcast(dtype)[:, :, c % 2 * QUARTER:(c % 2 + 1) * QUARTER]
+            copy(grp[c][:].bitcast(dtype).rearrange("p (c u) -> p c u", u=2), src.rearrange("p u c -> p c u"))
+
+        for c in range(3):
+            weave(c, nc.scalar.copy, U32)
+        weave(3, nc.vector.tensor_copy, I32)
+        for c in (0, 3, 1, 2):
             lo, hi = c * QUARTER, (c + 1) * QUARTER
-            src = grp[c // 2][:, c % 2 * QUARTER:(c % 2 + 1) * QUARTER]
-            nc.vector.quantize_mx(
-                out=codes[:, lo:hi].bitcast(FP8X4), scales=out_scales[:, lo:hi], in_=src.rearrange("p c t -> p (c t)")
-            )
-            if c > 0:
-                nc.sync.dma_start(words[:, stored:hi], codes[:, stored:hi].bitcast(I32))
-                stored = hi
+            nc.vector.quantize_mx(out=codes[:, lo:hi].bitcast(FP8X4), scales=out_scales[:, lo:hi], in_=grp[c][:])
+            nc.sync.dma_start(words[:, lo:hi], codes[:, lo:hi].bitcast(I32))
         for r in range(4):
             eng = nc.sync if r % 2 == 0 else nc.scalar
             eng.dma_start(out_2[0, r:16:4, :].bitcast(I32), out_scales[r:P:32, :].bitcast(I32))

@@ -72,7 +72,7 @@ def tile_picked_yham_euler_po_kernel(
         nc.sync.dma_start(bias_sb[:], bias.rearrange("(p t) o -> p (t o)", t=PACK))
         nc.sync.dma_start(w2_raw[:], w2.rearrange("(p j) c -> p j c", j=PACK))
         nc.sync.dma_start(top_sb[:], top.rearrange("(p t) o -> p (t o)", t=PACK))
-        for t in (1, 3, 2):
+        for t in (1, 2, 3):
             nc.sync.dma_start(y[t][:], mom_rows[t])
 
         def deal(raw, name, split, tag=None):
@@ -115,7 +115,6 @@ def tile_picked_yham_euler_po_kernel(
                         stop=(g == PASSES - 1),
                     )
 
-        pieces = [(0, HALF), (HALF, S)]
         old = [sb(f"old{t}", [P, S], F32) for t in range(PACK)]
         new = [sb(f"new{t}", [P, S], F32) for t in range(PACK)]
 
@@ -159,22 +158,16 @@ def tile_picked_yham_euler_po_kernel(
                 stop=True,
             )
 
-        def kick_out(t, i):
-            lo, hi = pieces[i]
-            nc.scalar.activation(new[t][:, lo:hi], acc2[t, i][:], ACT.Copy, scale=0.2)
+        def product(t, lo, hi):
+            return acc2[t, lo // HALF][:, lo % HALF:lo % HALF + hi - lo]
 
-        def kick_add(t, i):
-            lo, hi = pieces[i]
-            nc.vector.scalar_tensor_tensor(new[t][:, lo:hi], acc2[t, i][:], 0.2, old[t][:, lo:hi], ALU.mult, ALU.add)
+        def kick_add(t, lo, hi):
+            nc.vector.scalar_tensor_tensor(new[t][:, lo:hi], product(t, lo, hi), 0.2, old[t][:, lo:hi], ALU.mult, ALU.add)
 
-        def put_vector(t, i):
-            lo, hi = pieces[i]
-            nc.vector.tensor_tensor(
-                y[t][:].indirect(slot_sb[:, lo // 16:hi // 16]), old[t][:, lo:hi], new[t][:, lo:hi], ALU.add
-            )
+        def copy_vector(t, lo, hi):
+            nc.vector.tensor_copy(y[t][:].indirect(slot_sb[:, lo // 16:hi // 16]), new[t][:, lo:hi])
 
-        def put_scalar(t, i):
-            lo, hi = pieces[i]
+        def put_scalar(t, lo, hi):
             nc.scalar.activation(y[t][:].indirect(slot_sb[:, lo // 16:hi // 16]), new[t][:, lo:hi], ACT.Copy)
 
         def store(t):
@@ -186,10 +179,14 @@ def tile_picked_yham_euler_po_kernel(
             for c in range(2):
                 nc.vector.tensor_copy(pairs[c][:, t // 2, :, t % 2], y[t][:, c * COLS:(c + 1) * COLS])
 
+        def round_pool(t):
+            for c in range(2):
+                nc.gpsimd.tensor_scalar(pairs[c][:, t // 2, :, t % 2], y[t][:, c * COLS:(c + 1) * COLS], 1.0, -0.0, ALU.mult, ALU.add)
+
         fetch_vector(0)
         sq = [tanh_square(i) for i in range(2)]
         fetch_scalar(1)
-        fetch_scalar(3)
+        fetch_scalar(2)
         zq = {}
         w2_g = sb("w2_g", [P, PACK, P, PACK], BF16)
         nc.vector.tensor_copy(w2_g[:].rearrange("p t m j -> p m j t"), w2_raw[:].rearrange("p j (m t) -> p m j t", t=PACK))
@@ -201,32 +198,32 @@ def tile_picked_yham_euler_po_kernel(
         w2q.append(quant(w2_g[:, 2:4].rearrange("p t m j -> p (t m j)"), "w2q1", 2 * P))
         second(3, 0)
         second(2, 0)
-        kick_add(1, 0)
-        kick_out(0, 0)
-        put_scalar(1, 0)
-        fetch_scalar(2)
+        kick_add(1, 0, HALF)
+        put_scalar(1, 0, HALF)
         z_last = slope(1, sq[1])
-        kick_add(3, 0)
+        kick_add(0, 0, HALF)
+        put_scalar(0, 0, HALF)
+        fetch_scalar(3)
         zq[1] = quant(z_last[:].rearrange("p c t -> p (c t)"), "zq1", HALF)
         for t in (0, 1, 2, 3):
             second(t, 1)
-        put_vector(0, 0)
-        kick_out(0, 1)
-        kick_out(2, 0)
-        kick_add(1, 1)
-        kick_add(2, 1)
-        put_scalar(1, 1)
+        kick_add(2, 0, HALF)
+        copy_vector(2, 0, HALF)
+        kick_add(0, HALF, S)
+        kick_add(1, HALF, S)
+        put_scalar(1, HALF, S)
         store(1)
-        put_scalar(2, 1)
-        put_vector(0, 1)
+        copy_vector(0, HALF, S)
         store(0)
-        kick_add(3, 1)
-        put_scalar(3, 0)
-        put_scalar(3, 1)
-        round_plane(0)
-        round_plane(1)
-        put_vector(2, 0)
+        round_pool(0)
+        round_pool(1)
+        kick_add(3, 0, HALF)
+        kick_add(2, HALF, S)
+        kick_add(3, HALF, S)
+        copy_vector(2, HALF, S)
         store(2)
+        put_scalar(3, 0, HALF)
+        put_scalar(3, HALF, S)
         store(3)
         round_plane(2)
         round_plane(3)

@@ -161,8 +161,16 @@ def tile_picked_yham_euler_po_kernel(
         def product(t, lo, hi):
             return acc2[t, lo // HALF][:, lo % HALF:lo % HALF + hi - lo]
 
+        def kick_out(t, lo, hi):
+            nc.scalar.activation(new[t][:, lo:hi], product(t, lo, hi), ACT.Copy, scale=0.2)
+
         def kick_add(t, lo, hi):
             nc.vector.scalar_tensor_tensor(new[t][:, lo:hi], product(t, lo, hi), 0.2, old[t][:, lo:hi], ALU.mult, ALU.add)
+
+        def put_vector(t, lo, hi):
+            nc.vector.tensor_tensor(
+                y[t][:].indirect(slot_sb[:, lo // 16:hi // 16]), old[t][:, lo:hi], new[t][:, lo:hi], ALU.add
+            )
 
         def copy_vector(t, lo, hi):
             nc.vector.tensor_copy(y[t][:].indirect(slot_sb[:, lo // 16:hi // 16]), new[t][:, lo:hi])
@@ -173,15 +181,10 @@ def tile_picked_yham_euler_po_kernel(
         def store(t):
             nc.sync.dma_start(out_rows[t], y[t][:])
 
-        pairs = [sb(f"pairs{c}", [P, 2, COLS, 2], BF16) for c in range(2)]
+        pairs = sb("pairs", [P, 2, U, 2], BF16)
 
-        def round_plane(t):
-            for c in range(2):
-                nc.vector.tensor_copy(pairs[c][:, t // 2, :, t % 2], y[t][:, c * COLS:(c + 1) * COLS])
-
-        def round_pool(t):
-            for c in range(2):
-                nc.gpsimd.tensor_scalar(pairs[c][:, t // 2, :, t % 2], y[t][:, c * COLS:(c + 1) * COLS], 1.0, -0.0, ALU.mult, ALU.add)
+        def round_plane(t, lo, hi):
+            nc.vector.tensor_copy(pairs[:, t // 2, lo:hi, t % 2], y[t][:, lo:hi])
 
         fetch_vector(0)
         sq = [tanh_square(i) for i in range(2)]
@@ -199,34 +202,35 @@ def tile_picked_yham_euler_po_kernel(
         second(3, 0)
         second(2, 0)
         kick_add(1, 0, HALF)
+        kick_out(2, 0, HALF)
         put_scalar(1, 0, HALF)
         z_last = slope(1, sq[1])
         kick_add(0, 0, HALF)
         put_scalar(0, 0, HALF)
         fetch_scalar(3)
         zq[1] = quant(z_last[:].rearrange("p c t -> p (c t)"), "zq1", HALF)
-        for t in (0, 1, 2, 3):
+        for t in (2, 1, 0, 3):
             second(t, 1)
-        kick_add(2, 0, HALF)
-        copy_vector(2, 0, HALF)
-        kick_add(0, HALF, S)
-        kick_add(1, HALF, S)
-        put_scalar(1, HALF, S)
-        store(1)
-        copy_vector(0, HALF, S)
-        store(0)
-        round_pool(0)
-        round_pool(1)
-        kick_add(3, 0, HALF)
+        put_vector(2, 0, HALF)
         kick_add(2, HALF, S)
-        kick_add(3, HALF, S)
+        kick_add(1, HALF, S)
         copy_vector(2, HALF, S)
         store(2)
+        put_scalar(1, HALF, S)
+        store(1)
+        kick_add(0, HALF, S)
+        kick_add(3, 0, HALF)
+        kick_add(3, HALF, S)
+        copy_vector(0, HALF, S)
+        store(0)
         put_scalar(3, 0, HALF)
         put_scalar(3, HALF, S)
         store(3)
-        round_plane(2)
-        round_plane(3)
+        for t in (2, 0, 1):
+            round_plane(t, 0, U)
+        round_plane(PACK - 1, 0, QUARTER)
+        round_plane(PACK - 1, QUARTER, COLS)
+        round_plane(PACK - 1, COLS, U)
 
         out_scales = sb("out_scales", [P, U], U8)
         words = out_1[0].rearrange("p c r -> p (c r)").bitcast(I32)
@@ -234,16 +238,20 @@ def tile_picked_yham_euler_po_kernel(
         grp = [sb(f"grp{c}", [P, QUARTER * PACK], BF16) for c in range(4)]
 
         def weave(c, copy, dtype):
-            src = pairs[c // 2][:].rearrange("p u c e -> p u (c e)").bitcast(dtype)[:, :, c % 2 * QUARTER:(c % 2 + 1) * QUARTER]
+            src = pairs[:].rearrange("p u c e -> p u (c e)").bitcast(dtype)[:, :, c * QUARTER:(c + 1) * QUARTER]
             copy(grp[c][:].bitcast(dtype).rearrange("p (c u) -> p c u", u=2), src.rearrange("p u c -> p c u"))
 
-        for c in range(3):
-            weave(c, nc.scalar.copy, U32)
-        weave(3, nc.vector.tensor_copy, I32)
-        for c in (0, 3, 1, 2):
+        weave(0, nc.scalar.copy, U32)
+        weave(1, nc.vector.tensor_copy, I32)
+        weave(2, nc.scalar.copy, U32)
+        weave(3, nc.scalar.copy, U32)
+        stored = 0
+        for c in range(4):
             lo, hi = c * QUARTER, (c + 1) * QUARTER
             nc.vector.quantize_mx(out=codes[:, lo:hi].bitcast(FP8X4), scales=out_scales[:, lo:hi], in_=grp[c][:])
-            nc.sync.dma_start(words[:, lo:hi], codes[:, lo:hi].bitcast(I32))
+            if c > 0:
+                nc.sync.dma_start(words[:, stored:hi], codes[:, stored:hi].bitcast(I32))
+                stored = hi
         for r in range(4):
             eng = nc.sync if r % 2 == 0 else nc.scalar
             eng.dma_start(out_2[0, r:16:4, :].bitcast(I32), out_scales[r:P:32, :].bitcast(I32))

@@ -21,6 +21,7 @@ PASSES = K // (P * PACK)
 HALF = S // 2
 COLS = U // 2
 QUARTER = U // 4
+SHARE = 128
 
 
 def tile_picked_yham_euler_po_kernel(
@@ -116,7 +117,7 @@ def tile_picked_yham_euler_po_kernel(
                     )
 
         old = [sb(f"old{t}", [P, S], F32) for t in range(PACK)]
-        new = [sb(f"new{t}", [P, S], F32) for t in range(PACK)]
+        new = [sb(f"new{t}", [P, S], F32) for t in range(PACK - 1)]
 
         def fetch_vector(t):
             nc.vector.tensor_copy(old[t][:], y[t][:].indirect(slot_sb[:]))
@@ -186,6 +187,9 @@ def tile_picked_yham_euler_po_kernel(
         def round_plane(t, lo, hi):
             nc.vector.tensor_copy(pairs[:, t // 2, lo:hi, t % 2], y[t][:, lo:hi])
 
+        def round_pool(t):
+            nc.gpsimd.tensor_scalar(pairs[:, t // 2, :, t % 2], y[t][:], 1.0, -0.0, ALU.mult, ALU.add)
+
         fetch_vector(0)
         sq = [tanh_square(i) for i in range(2)]
         fetch_scalar(1)
@@ -199,35 +203,37 @@ def tile_picked_yham_euler_po_kernel(
         second(1, 0)
         second(0, 0)
         w2q.append(quant(w2_g[:, 2:4].rearrange("p t m j -> p (t m j)"), "w2q1", 2 * P))
-        second(3, 0)
         second(2, 0)
+        second(3, 0)
         kick_add(1, 0, HALF)
-        kick_out(2, 0, HALF)
+        kick_out(0, 0, HALF)
         put_scalar(1, 0, HALF)
         z_last = slope(1, sq[1])
-        kick_add(0, 0, HALF)
-        put_scalar(0, 0, HALF)
+        kick_add(2, 0, HALF)
+        put_scalar(2, 0, SHARE)
         fetch_scalar(3)
         zq[1] = quant(z_last[:].rearrange("p c t -> p (c t)"), "zq1", HALF)
-        for t in (2, 1, 0, 3):
+        for t in (1, 0, 2, 3):
             second(t, 1)
-        put_vector(2, 0, HALF)
-        kick_add(2, HALF, S)
+        put_vector(0, 0, HALF)
         kick_add(1, HALF, S)
-        copy_vector(2, HALF, S)
-        store(2)
+        kick_add(0, HALF, S)
         put_scalar(1, HALF, S)
         store(1)
-        kick_add(0, HALF, S)
-        kick_add(3, 0, HALF)
-        kick_add(3, HALF, S)
         copy_vector(0, HALF, S)
         store(0)
+        round_pool(0)
+        round_pool(1)
+        kick_add(2, HALF, S)
+        new.append(sb("new3", [P, S], F32, tag="old1"))
+        kick_add(3, 0, HALF)
+        kick_add(3, HALF, S)
+        copy_vector(2, SHARE, S)
+        store(2)
         put_scalar(3, 0, HALF)
         put_scalar(3, HALF, S)
         store(3)
-        for t in (2, 0, 1):
-            round_plane(t, 0, U)
+        round_plane(2, 0, U)
         round_plane(PACK - 1, 0, QUARTER)
         round_plane(PACK - 1, QUARTER, COLS)
         round_plane(PACK - 1, COLS, U)

@@ -117,7 +117,7 @@ def tile_picked_yham_euler_po_kernel(
                     )
 
         old = [sb(f"old{t}", [P, S], F32) for t in range(PACK)]
-        new = [sb(f"new{t}", [P, S], F32) for t in range(PACK - 1)]
+        new = [sb(f"new{t}", [P, S], F32) for t in range(2)]
 
         def fetch_vector(t):
             nc.vector.tensor_copy(old[t][:], y[t][:].indirect(slot_sb[:]))
@@ -209,24 +209,25 @@ def tile_picked_yham_euler_po_kernel(
         kick_out(0, 0, HALF)
         put_scalar(1, 0, HALF)
         z_last = slope(1, sq[1])
-        kick_add(2, 0, HALF)
-        put_scalar(2, 0, SHARE)
         fetch_scalar(3)
         zq[1] = quant(z_last[:].rearrange("p c t -> p (c t)"), "zq1", HALF)
-        for t in (1, 0, 2, 3):
+        for t in (0, 1, 2, 3):
             second(t, 1)
         put_vector(0, 0, HALF)
-        kick_add(1, HALF, S)
         kick_add(0, HALF, S)
-        put_scalar(1, HALF, S)
-        store(1)
-        copy_vector(0, HALF, S)
+        put_scalar(0, HALF, S)
         store(0)
+        kick_add(1, HALF, S)
+        new.append(sb("new2", [P, S], F32, tag="old0"))
+        kick_add(2, 0, HALF)
+        put_scalar(2, 0, SHARE)
+        copy_vector(1, HALF, S)
+        store(1)
         round_pool(0)
         round_pool(1)
-        kick_add(2, HALF, S)
         new.append(sb("new3", [P, S], F32, tag="old1"))
         kick_add(3, 0, HALF)
+        kick_add(2, HALF, S)
         kick_add(3, HALF, S)
         copy_vector(2, SHARE, S)
         store(2)

@@ -147,20 +147,20 @@ def tile_picked_yham_euler_po_kernel(
 
         acc2 = {}
 
-        def second(t, i):
-            acc2[t, i] = psum.tile([P, HALF], F32, name="acc")
+        def second(t, lo, hi):
+            acc2[t, lo] = psum.tile([P, hi - lo], F32, name="acc")
             nc.tensor.matmul_mx(
-                out=acc2[t, i][:],
+                out=acc2[t, lo][:],
                 lhsT=w2q[t // 2][0][:, t % 2 * P:(t % 2 + 1) * P].bitcast(FP8X4),
                 lhsT_scale=w2q[t // 2][1][:, t % 2 * P:(t % 2 + 1) * P],
-                rhs=zq[i][0][:].bitcast(FP8X4),
-                rhs_scale=zq[i][1][:],
+                rhs=z_codes[:, lo:hi].bitcast(FP8X4),
+                rhs_scale=z_scales[:, lo:hi],
                 start=True,
                 stop=True,
             )
 
         def product(t, lo, hi):
-            return acc2[t, lo // HALF][:, lo % HALF:lo % HALF + hi - lo]
+            return acc2[t, lo][:]
 
         def kick_out(t, lo, hi):
             nc.scalar.activation(new[t][:, lo:hi], product(t, lo, hi), ACT.Copy, scale=0.2)
@@ -194,41 +194,47 @@ def tile_picked_yham_euler_po_kernel(
         sq = [tanh_square(i) for i in range(2)]
         fetch_scalar(1)
         fetch_scalar(2)
-        zq = {}
+        z_codes = sb("z_codes", [P, S], U32)
+        z_scales = sb("z_scales", [P, S], U8)
+
+        def quant_z(i, z):
+            cols = slice(i * HALF, (i + 1) * HALF)
+            nc.vector.quantize_mx(
+                out=z_codes[:, cols].bitcast(FP8X4), scales=z_scales[:, cols], in_=z[:].rearrange("p c t -> p (c t)")
+            )
+
         w2_g = sb("w2_g", [P, PACK, P, PACK], BF16)
         nc.vector.tensor_copy(w2_g[:].rearrange("p t m j -> p m j t"), w2_raw[:].rearrange("p j (m t) -> p m j t", t=PACK))
         z_first = slope(0, sq[0])
         w2q = [quant(w2_g[:, 0:2].rearrange("p t m j -> p (t m j)"), "w2q0", 2 * P)]
-        zq[0] = quant(z_first[:].rearrange("p c t -> p (c t)"), "zq0", HALF)
-        second(1, 0)
-        second(0, 0)
+        quant_z(0, z_first)
+        second(1, 0, HALF)
+        second(0, 0, HALF)
         w2q.append(quant(w2_g[:, 2:4].rearrange("p t m j -> p (t m j)"), "w2q1", 2 * P))
-        second(2, 0)
-        second(3, 0)
         kick_add(1, 0, HALF)
         kick_out(0, 0, HALF)
         put_scalar(1, 0, HALF)
         z_last = slope(1, sq[1])
         fetch_scalar(3)
-        zq[1] = quant(z_last[:].rearrange("p c t -> p (c t)"), "zq1", HALF)
-        for t in (0, 1, 2, 3):
-            second(t, 1)
+        quant_z(1, z_last)
+        second(0, HALF, S)
+        second(1, HALF, S)
+        second(2, 0, S)
+        second(3, 0, S)
         put_vector(0, 0, HALF)
         kick_add(0, HALF, S)
         put_scalar(0, HALF, S)
         store(0)
         kick_add(1, HALF, S)
         new.append(sb("new2", [P, S], F32, tag="old0"))
-        kick_add(2, 0, HALF)
+        kick_add(2, 0, S)
         put_scalar(2, 0, SHARE)
+        new.append(sb("new3", [P, S], F32, tag="old1"))
+        kick_add(3, 0, S)
         copy_vector(1, HALF, S)
         store(1)
         round_pool(0)
         round_pool(1)
-        new.append(sb("new3", [P, S], F32, tag="old1"))
-        kick_add(3, 0, HALF)
-        kick_add(2, HALF, S)
-        kick_add(3, HALF, S)
         copy_vector(2, SHARE, S)
         store(2)
         put_scalar(3, 0, HALF)

@@ -22,6 +22,7 @@ HALF = S // 2
 COLS = U // 2
 QUARTER = U // 4
 SHARE = 128
+SQ_SCALAR = 16
 
 
 def tile_picked_yham_euler_po_kernel(
@@ -133,7 +134,8 @@ def tile_picked_yham_euler_po_kernel(
             dst = sq[:].rearrange("p (c i) t -> p c t i", i=4)
             src = h[:].rearrange("p t (c i) -> p c t i", i=4)
             if i == 0:
-                nc.vector.tensor_tensor(dst, src, src, ALU.mult)
+                nc.scalar.activation(dst[:, :SQ_SCALAR], src[:, :SQ_SCALAR], ACT.Square)
+                nc.vector.tensor_tensor(dst[:, SQ_SCALAR:], src[:, SQ_SCALAR:], src[:, SQ_SCALAR:], ALU.mult)
             else:
                 nc.scalar.activation(dst, src, ACT.Square)
             return sq

@@ -22,7 +22,7 @@ HALF = S // 2
 COLS = U // 2
 QUARTER = U // 4
 SHARE = 128
-SQ_SCALAR = 16
+SQ_SCALAR = 22
 
 
 def tile_picked_yham_euler_po_kernel(
@@ -133,12 +133,7 @@ def tile_picked_yham_euler_po_kernel(
             sq = sb(f"sq{i}", [P, HALF, PACK], F32)
             dst = sq[:].rearrange("p (c i) t -> p c t i", i=4)
             src = h[:].rearrange("p t (c i) -> p c t i", i=4)
-            if i == 0:
-                nc.scalar.activation(dst[:, :SQ_SCALAR], src[:, :SQ_SCALAR], ACT.Square)
-                nc.vector.tensor_tensor(dst[:, SQ_SCALAR:], src[:, SQ_SCALAR:], src[:, SQ_SCALAR:], ALU.mult)
-            else:
-                nc.scalar.activation(dst, src, ACT.Square)
-            return sq
+            return sq, dst, src
 
         def slope(i, sq):
             z = sb(f"z{i}", [P, HALF, PACK], BF16)
@@ -193,7 +188,12 @@ def tile_picked_yham_euler_po_kernel(
             nc.gpsimd.tensor_scalar(pairs[:, t // 2, :, t % 2], y[t][:], 1.0, -0.0, ALU.mult, ALU.add)
 
         fetch_vector(0)
-        sq = [tanh_square(i) for i in range(2)]
+        sq_first, dst, src = tanh_square(0)
+        nc.vector.tensor_tensor(dst[:, SQ_SCALAR:], src[:, SQ_SCALAR:], src[:, SQ_SCALAR:], ALU.mult)
+        sq_last, dst_last, src_last = tanh_square(1)
+        nc.scalar.activation(dst[:, :SQ_SCALAR], src[:, :SQ_SCALAR], ACT.Square)
+        nc.scalar.activation(dst_last, src_last, ACT.Square)
+        sq = [sq_first, sq_last]
         fetch_scalar(1)
         fetch_scalar(2)
         z_codes = sb("z_codes", [P, S], U32)

from contextlib import ExitStack

import concourse.mybir as mybir

K, T, S, H, N, U = 1024, 2048, 512, 512, 512, 1024
FLOPS = 2 * K * H * S + 2 * H * N * S

F32 = mybir.dt.float32
BF16 = mybir.dt.bfloat16
I32 = mybir.dt.int32
U32 = mybir.dt.uint32
U16 = mybir.dt.uint16
U8 = mybir.dt.uint8
FP8X4 = mybir.dt.float8_e4m3fn_x4
ALU = mybir.AluOpType
ACT = mybir.ActivationFunctionType

P = 128
PACK = 4
PASSES = K // (P * PACK)
HALF = S // 2
COLS = U // 2
QUARTER = U // 4
SHARE = 128
SQ_SCALAR = 22


def tile_picked_yham_euler_po_kernel(
    tc, x_words, x_scales, mom, w1, w2, bias, top, offs, slot, out_0, out_1, out_2
):
    nc = tc.nc
    with ExitStack() as ctx:
        keep = ctx.enter_context(tc.tile_pool(name="keep", bufs=1))
        psum = ctx.enter_context(tc.psum_pool(name="psum", bufs=8))

        def sb(name, shape, dtype, tag=None):
            return keep.tile(shape, dtype, name=name, tag=tag or name, align_bytes=64)

        offs_sb = keep.tile([P, S // 16], U16, name="offs_sb")
        slot_sb = keep.tile([P, S // 16], U16, name="slot_sb")
        xs_win = sb("xs_win", [P, T], U8)
        xw_win = [sb(f"xw_win{g}", [P, T], U32) for g in range(PASSES)]
        w1_raw = [sb(f"w1_raw{g}", [P, PACK, H], F32) for g in range(PASSES)]
        w2_raw = sb("w2_raw", [P, PACK, N], F32)
        y = [sb(f"y{t}", [P, U], F32) for t in range(PACK)]
        bias_sb = sb("bias_sb", [P, PACK], F32)
        top_sb = sb("top_sb", [P, PACK], F32)

        mom_rows = mom.rearrange("(p t) c -> t p c", t=PACK)
        out_rows = out_0.rearrange("(p t) c -> t p c", t=PACK)

        nc.vector.memset(xs_win[:].bitcast(I32), 0)

        def load_w1(g):
            nc.sync.dma_start(w1_raw[g][:], w1[g * 512:(g + 1) * 512, :].rearrange("(p j) c -> p j c", j=PACK))

        def load_words(g):
            nc.sync.dma_start(xw_win[g][:].bitcast(I32), x_words[g].rearrange("p c r -> p (c r)").bitcast(I32))

        def load_scales(rows):
            for r in rows:
                for g in range(PASSES):
                    nc.sync.dma_start(xs_win[4 * g + r:P:32, :].bitcast(I32), x_scales[g, r:16:4, :].bitcast(I32))

        load_w1(0)
        nc.sync.dma_start(offs_sb[:], offs)
        load_scales((0, 1))
        load_words(0)
        load_scales((2, 3))
        load_w1(1)
        load_words(1)
        nc.sync.dma_start(slot_sb[:], slot)
        nc.sync.dma_start(y[0][:], mom_rows[0])
        nc.sync.dma_start(bias_sb[:], bias.rearrange("(p t) o -> p (t o)", t=PACK))
        nc.sync.dma_start(w2_raw[:], w2.rearrange("(p j) c -> p j c", j=PACK))
        nc.sync.dma_start(top_sb[:], top.rearrange("(p t) o -> p (t o)", t=PACK))
        for t in (1, 2, 3):
            nc.sync.dma_start(y[t][:], mom_rows[t])

        def deal(raw, name, split, tag=None):
            grouped = sb(name, [P, PACK, P, PACK], BF16, tag=tag)
            dst = grouped[:].rearrange("p t m j -> p m j t")
            src = raw[:].rearrange("p j (m t) -> p m j t", t=PACK)
            if split > 0:
                nc.vector.tensor_copy(dst[:, :split], src[:, :split])
            nc.scalar.copy(dst[:, split:], src[:, split:])
            return grouped

        def quant(grouped2d, name, width):
            codes = sb(name + "_c", [P, width], U32)
            scales = sb(name + "_s", [P, width], U8)
            nc.vector.quantize_mx(out=codes[:].bitcast(FP8X4), scales=scales[:], in_=grouped2d)
            return codes, scales

        w1q = []
        xs = sb("xs", [P, S], U8)
        xw = {}
        acc1 = {}
        for g in range(PASSES):
            grouped = deal(w1_raw[g], f"w1_g{g}", 80)
            w1q.append(quant(grouped[:].rearrange("p t m j -> p (t m j)"), f"w1q{g}", H))
            if g == 0:
                nc.vector.tensor_copy(xs[:], xs_win[:].indirect(offs_sb[:]))
            for hf in range(2):
                xw[g, hf] = sb(f"xw{g}{hf}", [P, HALF], U32)
                nc.vector.tensor_copy(xw[g, hf][:], xw_win[g][:].indirect(offs_sb[:, hf * 16:(hf + 1) * 16]))
                for t in range(PACK):
                    if g == 0:
                        acc1[hf, t] = psum.tile([P, HALF], F32, name="acc")
                    nc.tensor.matmul_mx(
                        out=acc1[hf, t][:],
                        lhsT=w1q[g][0][:, t * P:(t + 1) * P].bitcast(FP8X4),
                        lhsT_scale=w1q[g][1][:, t * P:(t + 1) * P],
                        rhs=xw[g, hf][:].bitcast(FP8X4),
                        rhs_scale=xs[4 * g:P, hf * HALF:(hf + 1) * HALF],
                        start=(g == 0),
                        stop=(g == PASSES - 1),
                    )

        old = [sb(f"old{t}", [P, S], F32) for t in range(PACK)]
        new = [sb(f"new{t}", [P, S], F32) for t in range(2)]

        def fetch_vector(t):
            nc.vector.tensor_copy(old[t][:], y[t][:].indirect(slot_sb[:]))

        def fetch_scalar(t):
            nc.scalar.activation(old[t][:], y[t][:].indirect(slot_sb[:]), ACT.Copy)

        def tanh_square(i):
            h = sb(f"h{i}", [P, PACK, HALF], F32)
            for t in range(PACK):
                nc.scalar.activation(h[:, t, :], acc1[i, t][:], ACT.Tanh, bias=bias_sb[:, t:t + 1])
            sq = sb(f"sq{i}", [P, HALF, PACK], F32)
            dst = sq[:].rearrange("p (c i) t -> p c t i", i=4)
            src = h[:].rearrange("p t (c i) -> p c t i", i=4)
            return sq, dst, src

        def slope(i, sq):
            z = sb(f"z{i}", [P, HALF, PACK], BF16)
            nc.vector.scalar_tensor_tensor(
                z[:], sq[:], 1.0, top_sb[:].unsqueeze(1).to_broadcast([P, HALF, PACK]), ALU.subtract, ALU.mult
            )
            return z

        acc2 = {}

        def second(t, lo, hi):
            acc2[t, lo] = psum.tile([P, hi - lo], F32, name="acc")
            nc.tensor.matmul_mx(
                out=acc2[t, lo][:],
                lhsT=w2q[t // 2][0][:, t % 2 * P:(t % 2 + 1) * P].bitcast(FP8X4),
                lhsT_scale=w2q[t // 2][1][:, t % 2 * P:(t % 2 + 1) * P],
                rhs=z_codes[:, lo:hi].bitcast(FP8X4),
                rhs_scale=z_scales[:, lo:hi],
                start=True,
                stop=True,
            )

        def product(t, lo, hi):
            return acc2[t, lo][:]

        def kick_out(t, lo, hi):
            nc.scalar.activation(new[t][:, lo:hi], product(t, lo, hi), ACT.Copy, scale=0.2)

        def kick_add(t, lo, hi):
            nc.vector.scalar_tensor_tensor(new[t][:, lo:hi], product(t, lo, hi), 0.2, old[t][:, lo:hi], ALU.mult, ALU.add)

        def put_vector(t, lo, hi):
            nc.vector.tensor_tensor(
                y[t][:].indirect(slot_sb[:, lo // 16:hi // 16]), old[t][:, lo:hi], new[t][:, lo:hi], ALU.add
            )

        def copy_vector(t, lo, hi):
            nc.vector.tensor_copy(y[t][:].indirect(slot_sb[:, lo // 16:hi // 16]), new[t][:, lo:hi])

        def put_scalar(t, lo, hi):
            nc.scalar.activation(y[t][:].indirect(slot_sb[:, lo // 16:hi // 16]), new[t][:, lo:hi], ACT.Copy)

        def store(t):
            nc.sync.dma_start(out_rows[t], y[t][:])

        pairs = sb("pairs", [P, 2, U, 2], BF16)

        def round_plane(t, lo, hi):
            nc.vector.tensor_copy(pairs[:, t // 2, lo:hi, t % 2], y[t][:, lo:hi])

        def round_pool(t):
            nc.gpsimd.tensor_scalar(pairs[:, t // 2, :, t % 2], y[t][:], 1.0, -0.0, ALU.mult, ALU.add)

        fetch_vector(0)
        sq_first, dst, src = tanh_square(0)
        nc.vector.tensor_tensor(dst[:, SQ_SCALAR:], src[:, SQ_SCALAR:], src[:, SQ_SCALAR:], ALU.mult)
        sq_last, dst_last, src_last = tanh_square(1)
        nc.scalar.activation(dst[:, :SQ_SCALAR], src[:, :SQ_SCALAR], ACT.Square)
        nc.scalar.activation(dst_last, src_last, ACT.Square)
        sq = [sq_first, sq_last]
        fetch_scalar(1)
        fetch_scalar(2)
        z_codes = sb("z_codes", [P, S], U32)
        z_scales = sb("z_scales", [P, S], U8)

        def quant_z(i, z):
            cols = slice(i * HALF, (i + 1) * HALF)
            nc.vector.quantize_mx(
                out=z_codes[:, cols].bitcast(FP8X4), scales=z_scales[:, cols], in_=z[:].rearrange("p c t -> p (c t)")
            )

        w2_g = sb("w2_g", [P, PACK, P, PACK], BF16)
        nc.vector.tensor_copy(w2_g[:].rearrange("p t m j -> p m j t"), w2_raw[:].rearrange("p j (m t) -> p m j t", t=PACK))
        z_first = slope(0, sq[0])
        w2q = [quant(w2_g[:, 0:2].rearrange("p t m j -> p (t m j)"), "w2q0", 2 * P)]
        quant_z(0, z_first)
        second(1, 0, HALF)
        second(0, 0, HALF)
        w2q.append(quant(w2_g[:, 2:4].rearrange("p t m j -> p (t m j)"), "w2q1", 2 * P))
        kick_add(1, 0, HALF)
        kick_out(0, 0, HALF)
        put_scalar(1, 0, HALF)
        z_last = slope(1, sq[1])
        fetch_scalar(3)
        quant_z(1, z_last)
        second(0, HALF, S)
        second(1, HALF, S)
        second(2, 0, S)
        second(3, 0, S)
        put_vector(0, 0, HALF)
        kick_add(0, HALF, S)
        put_scalar(0, HALF, S)
        store(0)
        kick_add(1, HALF, S)
        new.append(sb("new2", [P, S], F32, tag="old0"))
        kick_add(2, 0, S)
        put_scalar(2, 0, SHARE)
        new.append(sb("new3", [P, S], F32, tag="old1"))
        kick_add(3, 0, S)
        copy_vector(1, HALF, S)
        store(1)
        round_pool(0)
        round_pool(1)
        copy_vector(2, SHARE, S)
        store(2)
        put_scalar(3, 0, HALF)
        put_scalar(3, HALF, S)
        store(3)
        round_plane(2, 0, U)
        round_plane(PACK - 1, 0, QUARTER)
        round_plane(PACK - 1, QUARTER, COLS)
        round_plane(PACK - 1, COLS, U)

        out_scales = sb("out_scales", [P, U], U8)
        words = out_1[0].rearrange("p c r -> p (c r)").bitcast(I32)
        codes = sb("out_codes", [P, U], U32)
        grp = [sb(f"grp{c}", [P, QUARTER * PACK], BF16) for c in range(4)]

        def weave(c, copy, dtype):
            src = pairs[:].rearrange("p u c e -> p u (c e)").bitcast(dtype)[:, :, c * QUARTER:(c + 1) * QUARTER]
            copy(grp[c][:].bitcast(dtype).rearrange("p (c u) -> p c u", u=2), src.rearrange("p u c -> p c u"))

        weave(0, nc.scalar.copy, U32)
        weave(1, nc.vector.tensor_copy, I32)
        weave(2, nc.scalar.copy, U32)
        weave(3, nc.scalar.copy, U32)
        stored = 0
        for c in range(4):
            lo, hi = c * QUARTER, (c + 1) * QUARTER
            nc.vector.quantize_mx(out=codes[:, lo:hi].bitcast(FP8X4), scales=out_scales[:, lo:hi], in_=grp[c][:])
            if c > 0:
                nc.sync.dma_start(words[:, stored:hi], codes[:, stored:hi].bitcast(I32))
                stored = hi
        for r in range(4):
            eng = nc.sync if r % 2 == 0 else nc.scalar
            eng.dma_start(out_2[0, r:16:4, :].bitcast(I32), out_scales[r:P:32, :].bitcast(I32))
